import numpy as np, ml_dtypes
CORES = [25,29,65,69,153,157,193,197]
N = 8
BF = ml_dtypes.bfloat16
def gentries(a):
    return np.ascontiguousarray(a.reshape(8, 16, -1).transpose(0, 2, 1)).reshape(8, -1)
def gtable(e):
    e = np.asarray(e); return np.ascontiguousarray(e.reshape(8, -1, 16).transpose(0, 2, 1)).reshape(128, -1).astype(np.int32)
V, R = 2048, 3
def family(rng, sizes, depth, pool, mix, fall=None):
    key = np.tile(np.arange(V), (N, 1)); lev = np.zeros(V, np.int64); comp = np.zeros(V, np.int64); via = [-1] * V; o = rng.permutation(V); a = 0
    for i in range(len(sizes)):
        s, D = int(sizes[i]), int(depth[i]); m = o[a:a + s]; a += s; comp[m] = i
        if s == 1: continue
        root = int(np.min(m)); m = m[m != root]; l = np.concatenate([np.arange(1, D + 1), rng.integers(1, D + 1, s - 1 - D)])
        if fall is not None and fall[i]: m = np.sort(m)[::-1]; l = np.sort(l)
        lev[m] = l
        at = [[root]] + [[] for k in range(D)]
        for c, k in zip(m.tolist(), l.tolist()): at[k].append(c)
        for k in range(1, D + 1):
            for c in at[k]:
                p = at[k - 1][int(rng.integers(len(at[k - 1])))]; w = [q for q in pool if q != via[p]]; q = w[int(rng.integers(len(w)))]
                key[q, c] = key[q, p]; via[c] = q
    for q in range(N if mix > 0 else 0):
        h = np.flatnonzero(key[q] == np.arange(V)); t = comp[h] * (R + 1) + lev[h]; keep = rng.random(h.size) >= mix
        hk, tk = h[keep], t[keep]; s = np.argsort(tk, kind="stable"); hk, tk = hk[s], tk[s]
        lo = np.searchsorted(tk, t, "left"); n = np.searchsorted(tk, t, "right") - lo; z = ~keep & (n > 0)
        to = h + 0; to[z] = hk[lo[z] + (rng.random(np.count_nonzero(z)) * n[z]).astype(np.int64)]
        jump = np.arange(V); jump[h] = to; key[q] = jump[key[q]]
    return key
def lay(rng, key, way):
    if way == 0: o = np.lexsort((rng.random(V), rng.permutation(V)[key]))
    elif way == 1: o = np.lexsort((np.arange(V), key))
    else: o = np.lexsort((-np.arange(V), -key))
    k = key[o]; s = np.ones(V, np.int64); s[1:] = k[1:] != k[:-1]
    e = np.append(np.flatnonzero(s)[1:], V) - 1; last = np.zeros(V, np.int64); last[o] = e[np.add.accumulate(s) - 1]
    return [o, s, last]
def pack(rng, keys, ways):
    a = np.array([[lay(rng, keys[g][q], ways[q, g]) for g in range(8)] for q in range(N)])
    return {"pm": np.stack([gtable(u) for u in a[:, :, 0]]), "en": np.stack([gtable(u) for u in a[:, :, 2]]), "st": np.ascontiguousarray(a[:, :, 1]).astype(np.int32)}
def depths(rng, s):
    top = np.minimum(R, s - 1); D = np.where(top > 0, 1 + (rng.random(s.size) * top).astype(np.int64), 0); i = np.argmax(s); D[i] = top[i]; return D
def some(rng):
    out = []
    for n in rng.choice(np.arange(6, 41), 8, replace=False):
        c = np.sort(rng.choice(V - 1, int(n) - 1, replace=False)) + 1; s = np.diff(np.concatenate([[0], c, [V]]))
        out.append(family(rng, s, depths(rng, s), list(range(N)), rng.choice([0.0, 0.05, 0.15])))
    return out
def setup_inputs(rng):
    return pack(rng, some(rng), np.zeros((N, 8), np.int64))
def setup_inputs_deep(rng):
    few = rng.permutation(8)[:4]; n = rng.choice(np.arange(V // (2 * (R + 1)), V // (R + 1) + 1), 8, replace=False); keys = []
    for g in range(8):
        m = int(n[g]); s = [R + 1] * m + [1] * (V - m * (R + 1)); pool = rng.permutation(N)[:2].tolist() if g in few else list(range(N))
        keys.append(family(rng, s, [R] * m + [0] * (V - m * (R + 1)), pool, 0.0, np.arange(len(s)) % 2 == 0))
    return pack(rng, keys, np.zeros((N, 8), np.int64))
def setup_inputs_ends(rng):
    keys = some(rng); w = rng.permutation(8); one = np.tile(np.arange(V), (N, 1))
    keys[w[0]][rng.integers(N)] = 0
    keys[w[1]] = one + 0
    keys[w[2]] = np.tile(rng.integers(0, 30, V), (N, 1))
    keys[w[3]] = one + 0; keys[w[3]][rng.integers(N)] = rng.integers(0, 3, V)
    x = np.concatenate([[0], 1 + rng.choice(V - 2, R - 1, replace=False), [V - 1]]); k = one + 0; ab = rng.permutation(N)[:2]
    for i in range(R): k[ab[i % 2], x[i + 1]] = x[i]
    keys[w[4]] = k
    return pack(rng, keys, np.zeros((N, 8), np.int64))
def setup_inputs_order(rng):
    return pack(rng, some(rng), rng.integers(1, 3, (N, 8)))
def setup_inputs_spread(rng):
    keys = []; half = int(rng.integers(8))
    for g in range(8):
        s = [1] * (V // 2 if g == half else 0); left = V - len(s)
        while left > 0:
            t = max(1, int(left * (0.3 + 0.4 * rng.random()))); s.append(t); left -= t
        s = np.array(s); keys.append(family(rng, s, depths(rng, s), list(range(N)) + [int(rng.integers(N))] * (3 * N), rng.choice([0.0, 0.3, 0.8])))
    return pack(rng, keys, np.zeros((N, 8), np.int64))
def hop(p, st, L):
    g = np.arange(8)[:, None]; M = L
    for q in range(N):
        s = st[q].reshape(-1); m = np.minimum.reduceat(L[g, p[q]].reshape(-1), np.flatnonzero(s))
        u = np.empty_like(L); u[g, p[q]] = m[np.add.accumulate(s) - 1].reshape(8, V); M = np.minimum(M, u)
    return M
def check_inputs(d):
    p = np.stack([gentries(a) for a in d["pm"]]); e = np.stack([gentries(a) for a in d["en"]]); s = d["st"]
    if not (np.sort(p, -1) == np.arange(V)).all(): return ["pm: every vertex once"]
    if not (((s == 0) | (s == 1)).all() and (s[:, :, 0] == 1).all()): return ["st: 0 and 1, beginning with 1"]
    bad = []; t = s.reshape(-1); last = ((np.append(np.flatnonzero(t)[1:], t.size) - 1) % V)[np.add.accumulate(t) - 1].reshape(N, 8, V)
    if not (np.take_along_axis(e, p, 2) == last).all(): bad.append("en: last places")
    L = np.tile(np.arange(V), (8, 1))
    for i in range(R): L = hop(p, s, L)
    if not (hop(p, s, L) == L).all(): bad.append("at most R steps to the smallest vertex")
    return bad
def reference(pm, en, st):
    p = np.stack([gentries(a) for a in pm]); L = np.tile(np.arange(V), (8, 1))
    while True:
        M = hop(p, st, L)
        if (M == L).all(): break
        L = M
    c = np.count_nonzero(L == np.arange(V), axis=1).reshape(8, 1)
    return {"y": np.stack([L[:, r * 256:(r + 1) * 256] for r in range(N)]).astype(np.float32), "cnt": np.stack([c for r in range(N)]).astype(np.float32)}

@@ -1,0 +1,349 @@
+from concourse.bass import DstId, RemoteDMATransfer
+from concourse.mybir import AluOpType as A, ActivationFunctionType as F
+
+V = 2048
+XA, XB = 768, 1472
+SC = 2.0 ** -15
+BASE = [-16384, -8192, -4096, -2048, -1024, -512, -256, -128, 0, 128, 256, 512, 1024, 2048, 4096, 8192]
+SLOPE = [64, 32, 16, 8, 4, 2, 1, 1, 1, 1, 2, 4, 8, 16, 32, 64]
+KNOTS = [256, 512, 1024, 2048, 4096, 8192]
+WEIGHT = [2.0 ** (14 - j) for j in range(6)] + [2.0 ** 9]
+
+SCRATCH = {
+    "pmi": ("sbuf", [128, 128], "int32"), "eni": ("sbuf", [128, 128], "int32"),
+    "w1p": ("sbuf", [128, 128], "uint16"), "w1e": ("sbuf", [128, 128], "uint16"),
+    "w2p": ("sbuf", [128, 128], "uint16"), "w2e": ("sbuf", [128, 128], "uint16"),
+    "p2i": ("sbuf", [128, 128], "int32"), "e2i": ("sbuf", [128, 128], "int32"),
+    "first": ("sbuf", [128, V], "bfloat16"),
+    "base": ("sbuf", [128, 128], "bfloat16"), "ones": ("sbuf", [128, 128], "bfloat16"),
+    "ident": ("sbuf", [128, 128], "bfloat16"), "pick": ("sbuf", [128, 8], "bfloat16"),
+    "reset": ("sbuf", [128, 128], "bfloat16"), "keep": ("sbuf", [128, 128], "bfloat16"),
+    "wid": ("sbuf", [128, 7 * 128], "bfloat16"), "own": ("sbuf", [128, 128], "bfloat16"),
+    "pint": ("sbuf", [128, 16], "int32"), "pmod": ("sbuf", [128, 16], "int32"), "phalf": ("sbuf", [128, 16], "int32"),
+    "podd": ("sbuf", [128, 16], "int32"), "psum2": ("sbuf", [128, 16], "int32"),
+    "off1": ("sbuf", [128, 10], "uint16"), "off8": ("sbuf", [128, 10], "uint16"), "offy": ("sbuf", [128, 2], "uint16"),
+    "win1": ("sbuf", [128, V], "bfloat16"), "win2": ("sbuf", [128, V], "bfloat16"), "win3": ("sbuf", [128, V], "bfloat16"),
+    "x1": ("sbuf", [128, V], "bfloat16"), "x2": ("sbuf", [128, V], "bfloat16"), "x3": ("sbuf", [128, V], "bfloat16"),
+    "s1": ("sbuf", [128, V], "bfloat16"), "s2": ("sbuf", [128, V], "bfloat16"), "s3": ("sbuf", [128, V], "bfloat16"),
+    "u1": ("sbuf", [128, V], "bfloat16"), "u2": ("sbuf", [128, V], "bfloat16"), "u3": ("sbuf", [128, V], "bfloat16"),
+    "mine": ("sbuf", [128, 128], "bfloat16"), "landd": ("sbuf", [128, 48], "bfloat16"), "landr": ("sbuf", [128, 64], "bfloat16"),
+    "ea": ("sbuf", [128, 32], "bfloat16"), "ra": ("sbuf", [128, 32], "bfloat16"), "rb": ("sbuf", [128, 32], "bfloat16"),
+    "m1": ("sbuf", [128, 16], "bfloat16"), "m2": ("sbuf", [128, 128], "bfloat16"), "m3": ("sbuf", [128, 128], "bfloat16"),
+    "b1": ("sbuf", [128, 144], "bfloat16"), "b2": ("sbuf", [128, 144], "bfloat16"),
+    "ytile": ("sbuf", [128, 16], "bfloat16"), "landy": ("sbuf", [128, 128], "bfloat16"),
+    "cl": ("sbuf", [128, 7 * 16], "bfloat16"), "eq": ("sbuf", [128, 128], "bfloat16"),
+    "yrow": ("sbuf", [128, 128], "float32"), "crun": ("sbuf", [128, 128], "float32"), "crow": ("sbuf", [128, 8], "float32"),
+    "hu": ("sbuf", [128, 32], "bfloat16"), "hy": ("sbuf", [128, 16], "bfloat16"),
+    "lp": ("dram", [8, 128, 16], "int32"), "le": ("dram", [8, 128, 16], "int32"), "ls": ("dram", [8, 128, 16], "int32"),
+    "dp": ("dram", [8, 128, 16], "int32"), "de": ("dram", [8, 128, 16], "int32"), "ds": ("dram", [8, 128, 16], "int32"),
+    "hp": ("dram", [2, 128, 16], "int32"), "he": ("dram", [2, 128, 16], "int32"), "hs": ("dram", [2, 128, 16], "int32"),
+    "psb": ("psum", [128, V], "float32"),
+    "ps1": ("psum", [128, 512], "float32"), "ps2": ("psum", [128, 512], "float32"), "ps3": ("psum", [128, 512], "float32"),
+    "psy": ("psum", [128, 512], "float32"),
+}
+NT = 128
+SEMAPHORES = ["t%d" % i for i in range(NT)] + ["alist", "astart", "adir", "arel", "aydir", "ayrel", "hlist", "hstart", "hlab", "hfin"]
+
+
+def runner(g, T):
+    Q = {"g": g, "v": g.vector, "s": g.scalar, "p": g.tensor, "y": g.sync}
+    tags, know, count = {}, {k: set() for k in Q}, [0]
+
+    def tag(name, sem=None, n=0):
+        if name not in tags:
+            if sem is None:
+                sem = "t%d" % count[0]
+                count[0] += 1
+            tags[name] = {"sem": sem, "n": n, "know": set(), "waited": False}
+        return tags[name]
+
+    def wait(q, after):
+        for a in after:
+            if a in know[q]:
+                continue
+            t = tags[a]
+            Q[q].wait_ge(T.sem[t["sem"]], t["n"])
+            t["waited"] = True
+            know[q] |= {a} | t["know"]
+
+    def raised(q, name, n):
+        t = tag(name)
+        assert not t["waited"], name
+        t["n"] += n
+        t["know"] |= know[q]
+        return T.sem[t["sem"]]
+
+    def op(q, name, after, call, n=1, **kw):
+        wait(q, after)
+        call(**kw).then_inc(raised(q, name, n), n)
+
+    def dma(q, name, after, out, in_):
+        wait(q, after)
+        Q[q].dma_start(out=out, in_=in_).then_inc(raised(q, name, 16), 16)
+
+    def send(name, after, jobs, rsem, topo, core):
+        wait("g", after)
+        tr, total = [], 0
+        for dst, out, src, eng in jobs:
+            rid, pid = topo.addr(dst, core)
+            tr.append(RemoteDMATransfer(dst_ids=[DstId(rid=rid, pnc=pid)], dma_engine_mask=sum(1 << e for e in eng),
+                                        remote_sem=T.sem[rsem], src=src, dst=out))
+            total += len(eng)
+        g.remote_dma_fused(tr, local_sem=raised("g", name, total))
+
+    def finish():
+        wait("g", [a for a in tags if not tags[a]["waited"]])
+
+    return {"tag": tag, "wait": wait, "op": op, "dma": dma, "send": send, "finish": finish}
+
+
+def plan(T, topo):
+    cores = T.cores
+    near = [[p for p in range(len(cores)) if cores[p] in topo.cores_of(cores[q]) or topo.same_plane(cores[q], cores[p])]
+            for q in range(len(cores))]
+    owners = near[0] + [p for p in range(len(cores)) if p not in near[0]]
+    group = {p: k for k, p in enumerate(owners)}
+    return cores, near, owners, group
+
+
+def helpers(T, topo, q, far):
+    c = T.cores[q]
+    return [h for h in topo.cores_of(c) if T.rank_of(h) is None and topo.die(h) == topo.die(c)
+            and all(topo.may_write(h, T.cores[d]) for d in far)][:2]
+
+
+def helper_program(g, core, T, topo, q, far, mine):
+    r = runner(g, T)
+    cores, near, owners, group = plan(T, topo)
+    dst = [cores[d] for d in mine]
+    e = topo.engines(core, dst[0])
+    slot = near[mine[0]]
+    fr = [p for p in range(len(cores)) if p not in slot]
+    s = fr.index(q)
+    h = len(e) // 2
+    k = len(e) // 4
+    r["tag"]("hlist", "hlist", 4)
+    r["tag"]("hstart", "hstart", 4)
+    r["tag"]("hlab", "hlab", 8)
+    r["tag"]("hfin", "hfin", 8)
+    jobs = []
+    for i in range(2):
+        jobs.append((dst[i], T.dp[q], T.hp[i], e[2 * i * k:(2 * i + 1) * k]))
+        jobs.append((dst[i], T.de[q], T.he[i], e[(2 * i + 1) * k:(2 * i + 2) * k]))
+    r["send"]("fl", ["hlist"], jobs, "alist", topo, core)
+    r["send"]("fs", ["hstart"], [(dst[i], T.ds[q], T.hs[i], e[h * i:h * i + h]) for i in range(2)], "astart", topo, core)
+    r["send"]("fu", ["hlab"], [(dst[i], T.landr[:, 16 * s:16 * s + 16], T.hu[:, 16 * i:16 * i + 16], e[h * i:h * i + h])
+                               for i in range(2)], "arel", topo, core)
+    r["send"]("fy", ["hfin"], [(dst[i], T.landy[:, 16 * group[q]:16 * group[q] + 16], T.hy[:], e[h * i:h * i + h])
+                               for i in range(2)], "ayrel", topo, core)
+    r["finish"]()
+
+
+def rank_program(g, core, T, topo):
+    cores, near, owners, group = plan(T, topo)
+    rank = T.rank_of(core)
+    if rank is None:
+        for q in range(len(cores)):
+            if core in topo.cores_of(cores[q]):
+                far = [d for d in owners if d not in near[q]]
+                hs = helpers(T, topo, q, far)
+                if core in hs:
+                    i = hs.index(core)
+                    helper_program(g, core, T, topo, q, far, far[2 * i:2 * i + 2])
+        return
+    R = runner(g, T)
+    op, dma, send, tag, wait = R["op"], R["dma"], R["send"], R["tag"], R["wait"]
+    v, s, p = g.vector, g.scalar, g.tensor
+    go = group[rank]
+    far = [d for d in owners if d not in near[rank]]
+    hs = helpers(T, topo, rank, far)
+    mate = [d for d in near[rank] if d != rank and cores[d] in topo.cores_of(core)][0]
+    plane = [d for d in near[rank] if d != rank and d != mate]
+    off = topo.engines(core, cores[plane[0]])
+    allr = topo.engines(core, hs[0])
+    on = [x for x in allr if x not in off]
+    for nm, n in (("alist", 24), ("astart", 24), ("adir", 16), ("arel", 16), ("aydir", 16), ("ayrel", 16)):
+        tag(nm, nm, n)
+
+    def slot(d):
+        return [x for x in near[d] if x != d].index(rank)
+
+    dma("y", "pm", [], T.pmi[:], T.pm[:])
+    dma("s", "en", [], T.eni[:], T.en[:])
+    dma("y", "lpe", [], T.lp[:], T.pm[:])
+    dma("s", "lpe", [], T.le[:], T.en[:])
+    dma("y", "ls", [], T.ls[:], T.st[:])
+    dma("y", "ownl", [], T.dp[rank], T.pm[16 * go:16 * go + 16, :])
+    dma("y", "ownl", [], T.de[rank], T.en[16 * go:16 * go + 16, :])
+    dma("y", "owns", [], T.ds[rank], T.st[go:go + 1, :])
+
+    op("g", "base", [], g.iota, out=T.base[:], pattern=[[1, 128]], base=0, channel_multiplier=0,
+       allow_small_or_imprecise_dtypes=True)
+    op("v", "mfirst", [], v.memset, ap=T.first[:], constant=0.0)
+    op("v", "ones", [], v.memset, ap=T.ones[:], constant=1.0)
+    wait("g", ["mfirst"])
+    dma("g", "d1", ["mfirst"], T.first[0:128:16, :], T.st[:])
+    for i in range(16):
+        o = T.win1[:, 128 * i:128 * i + 128]
+        if i % 8 < 5:
+            op("v", "win1", ["base"], v.tensor_scalar, out=o, in0=T.base[:], scalar1=SLOPE[i] * SC, scalar2=BASE[i] * SC,
+               op0=A.mult, op1=A.add)
+        else:
+            op("s", "win1", ["base"], s.activation, out=o, in_=T.base[:], func=F.Identity, scale=SLOPE[i] * SC, bias=0.0) \
+                if BASE[i] == 0 else op("s", "win1", ["base"], s.activation, out=o, in_=T.base[:], func=F.Copy,
+                                        scale=SLOPE[i] * SC, bias=BASE[i] * SC)
+    op("g", "pick", ["ones"], g.affine_select, out=T.pick[:], in_=T.ones[:, 0:8], pattern=[[-16, 8]], compare_op=A.is_equal,
+       fill=0.0, base=0, channel_multiplier=1)
+    jobs = []
+    for i, d in enumerate(far):
+        jobs.append((hs[i // 2], T.hp[i % 2], T.lp[group[d]], [on[2 * i]]))
+        jobs.append((hs[i // 2], T.he[i % 2], T.le[group[d]], [on[2 * i + 1]]))
+    direct = [(plane[0], off[0:1], off[1:2]), (plane[1], off[2:3], off[3:4]), (mate, off[4:6], off[6:8])]
+    toh = jobs
+    tod = []
+    for d, ea, eb in direct:
+        tod.append((cores[d], T.dp[rank], T.lp[group[d]], ea))
+        tod.append((cores[d], T.de[rank], T.le[group[d]], eb))
+    wait("g", ["lpe"])
+    send_two(R, T, g, topo, core, "cl1", [(toh, "hlist"), (tod, "alist")])
+    wait("g", ["ls"])
+    toh = [(hs[i // 2], T.hs[i % 2], T.ls[group[d]], on[2 * i:2 * i + 2]) for i, d in enumerate(far)]
+    tod = [(cores[d], T.ds[rank], T.ls[group[d]], ea + eb) for d, ea, eb in direct]
+    send_two(R, T, g, topo, core, "cl2", [(toh, "hstart"), (tod, "astart")])
+
+    def step(h, win, wp, we, ready, x, sc, u, ps, first, extra):
+        n = lambda t: t + str(h)
+        op("v", n("ga"), ready + [wp[1]], v.tensor_copy, out=x[:, 0:XA], in_=win[:, 0:V].indirect(wp[0][:, 0:XA // 16]))
+        op("s", n("gb"), ready + [wp[1]], s.activation, out=x[:, XA:XB], in_=win[:, 0:V].indirect(wp[0][:, XA // 16:XB // 16]),
+           func=F.Copy)
+        op("s", n("gc"), ready, s.activation, out=x[:, XB:V], in_=win[:, 0:V].indirect(wp[0][:, XB // 16:V // 16]), func=F.Copy)
+        extra()
+        last = None
+        for a, b, t in ((0, XA, "ga"), (XA, XB, "gb"), (XB, V, "gc")):
+            op("v", n("sc" + t), [n(t), first] + ([last] if last else []), v.tensor_tensor_scan, out=sc[:, a:b],
+               data0=T.first[:, a:b], data1=x[:, a:b], initial=0.0 if a == 0 else sc[:, a - 1:a], op0=A.add, op1=A.min)
+            last = n("sc" + t)
+        parts = (("v", 0, 768), ("s", 1024, 1792), ("v", 768, 1024), ("s", 1792, 2048))
+        for q, a, b in parts:
+            o, i_ = u[:, a:b], sc[:, 0:V].indirect(we[0][:, a // 16:b // 16])
+            if q == "v":
+                op("v", n("u%d" % a), [last, we[1]], v.tensor_copy, out=o, in_=i_)
+            else:
+                op("s", n("u%d" % a), [last, we[1]], s.activation, out=o, in_=i_, func=F.Copy)
+        for q, a, b in parts:
+            for i in range(a // 128, b // 128):
+                o = ps[:, i:128:16] if h == 1 else ps[:, 8 * i:8 * i + 8]
+                op("p", n("sel"), [n("u%d" % a), "pick"], p.matmul, out=o, lhsT=u[:, 128 * i:128 * i + 128], rhs=T.pick[:],
+                   start=True, stop=True)
+
+    op("v", "w1p", ["pm"], v.tensor_copy, out=T.w1p[:], in_=T.pmi[:])
+    step(1, T.win1, (T.w1p, "w1p"), (T.w1e, "w1e"), ["win1"], T.x1, T.s1, T.u1, T.ps1, "d1",
+         lambda: op("v", "w1e", ["en"], v.tensor_copy, out=T.w1e[:], in_=T.eni[:]))
+    fa = 16 * group[far[0]]
+    na = 64 - fa
+    op("v", "minef", ["sel1"], v.tensor_copy, out=T.mine[:, fa:fa + 64], in_=T.ps1[:, fa:fa + 64])
+    op("v", "minen", ["sel1"], v.tensor_copy, out=T.mine[:, na:na + 64], in_=T.ps1[:, na:na + 64])
+    send("sf", ["minef"], [(hs[i], T.hu[:], T.mine[:, fa + 32 * i:fa + 32 * i + 32], allr[8 * i:8 * i + 8]) for i in range(2)],
+         "hlab", topo, core)
+    tod = [(mate, on), (plane[0], off[0:4]), (plane[1], off[4:8])]
+    send("sn", ["minen"], [(cores[d], T.landd[:, 16 * slot(d):16 * slot(d) + 16],
+                            T.mine[:, 16 * group[d]:16 * group[d] + 16], e) for d, e in tod], "adir", topo, core)
+    dma("g", "d2", ["astart", "owns", "scgc1"], T.first[0:128:16, :], T.ds[:])
+    op("g", "ident", ["ones"], g.affine_select, out=T.ident[:], in_=T.ones[:], pattern=[[-1, 128]], compare_op=A.is_equal,
+       fill=0.0, base=0, channel_multiplier=1)
+    op("g", "reset", ["ones"], g.affine_select, out=T.reset[:], in_=T.ones[:], pattern=[[0, 16], [1, 8]],
+       compare_op=A.is_equal, fill=0.0, base=0, channel_multiplier=0)
+    op("g", "pint", [], g.iota, out=T.pint[:], pattern=[[0, 16]], base=0, channel_multiplier=1)
+
+    dma("y", "p2i", ["alist", "ownl"], T.p2i[:], T.dp[:])
+    dma("y", "e2i", ["alist", "ownl"], T.e2i[:], T.de[:])
+    op("v", "pmod", ["pint"], v.tensor_scalar, out=T.pmod[:], in0=T.pint[:], scalar1=15, scalar2=None, op0=A.bitwise_and)
+    op("v", "off1", ["pmod"], v.tensor_scalar, out=T.off1[:], in0=T.pmod[:, 0:10], scalar1=1, scalar2=None, op0=A.mult)
+    op("v", "off8", ["pmod"], v.tensor_scalar, out=T.off8[:], in0=T.pmod[:, 0:10], scalar1=8, scalar2=7, op0=A.mult, op1=A.add)
+    op("v", "podd", ["pmod"], v.tensor_scalar, out=T.podd[:], in0=T.pmod[:], scalar1=1, scalar2=None, op0=A.bitwise_and)
+    op("v", "phalf", ["podd"], v.tensor_scalar, out=T.phalf[:], in0=T.pmod[:], scalar1=8, scalar2=2 * rank, op0=A.mult,
+       op1=A.add)
+    op("v", "podd7", ["podd"], v.tensor_scalar, out=T.psum2[:], in0=T.podd[:], scalar1=7, scalar2=None, op0=A.mult)
+    op("v", "podd8", ["podd7", "phalf"], v.tensor_tensor, out=T.podd[:], in0=T.phalf[:], in1=T.psum2[:], op=A.subtract)
+    op("v", "offy", ["podd8"], v.tensor_scalar, out=T.offy[:], in0=T.podd[:, 0:2], scalar1=1, scalar2=None, op0=A.mult)
+    op("v", "keep0", [], v.memset, ap=T.keep[:], constant=1.0)
+    op("v", "keep", ["keep0"], v.memset, ap=T.keep[:, 0:128:16], constant=0.0)
+    for j in range(7):
+        op("s", "wid", ["ident"], s.activation, out=T.wid[:, 128 * j:128 * j + 128], in_=T.ident[:], func=F.Copy,
+           scale=WEIGHT[j])
+    for i in range(16):
+        op("p", "qown", ["win1", "pick"], p.matmul, out=T.psy[:, i:128:16], lhsT=T.win1[:, 128 * i:128 * i + 128],
+           rhs=T.pick[:], start=True, stop=True)
+    op("s", "own", ["qown"], s.activation, out=T.own[:], in_=T.psy[:, 0:128], func=F.Copy)
+    op("v", "w2p", ["p2i"], v.tensor_copy, out=T.w2p[:], in_=T.p2i[:])
+    op("v", "w2e", ["e2i"], v.tensor_copy, out=T.w2e[:], in_=T.e2i[:])
+
+    og = 16 * go
+    op("v", "ea", ["adir"], v.tensor_tensor, out=T.ea[:, 0:16], in0=T.landd[:, 0:16], in1=T.landd[:, 16:32], op=A.min)
+    op("v", "ea", ["minen"], v.tensor_tensor, out=T.ea[:, 16:32], in0=T.landd[:, 32:48], in1=T.mine[:, og:og + 16], op=A.min)
+    op("v", "ra", ["arel"], v.tensor_tensor, out=T.ra[:], in0=T.landr[:, 0:32], in1=T.landr[:, 32:64], op=A.min)
+    op("v", "rb", ["ra", "ea"], v.tensor_tensor, out=T.rb[:], in0=T.ra[:], in1=T.ea[:], op=A.min)
+    op("v", "m1", ["rb"], v.tensor_tensor, out=T.m1[:], in0=T.rb[:, 0:16], in1=T.rb[:, 16:32], op=A.min)
+
+    def spread(h, src, n, offs, b, win, free):
+        op("v", "rep%d" % h, [src[1], offs[1]], v.tensor_copy, out=b[:], in_=src[0][:, 0:n].indirect(offs[0][:, 0:9]))
+        out = []
+        for k in range(4):
+            for i in range(4 * k, 4 * k + 4):
+                op("p", "row%d%d" % (h, k), ["rep%d" % h, "ident"] + free, p.matmul, out=T.psb[:, 128 * i:128 * i + 128],
+                   lhsT=b[:, i:i + 128], rhs=T.ident[:], start=True, stop=True)
+            o, i_ = win[:, 512 * k:512 * k + 512], T.psb[:, 512 * k:512 * k + 512]
+            t = "w%d%d" % (h, k)
+            if k % 2:
+                op("v", t, ["row%d%d" % (h, k)], v.tensor_copy, out=o, in_=i_)
+            else:
+                op("s", t, ["row%d%d" % (h, k)], s.activation, out=o, in_=i_, func=F.Copy)
+            out.append(t)
+        return out
+
+    ready = spread(2, (T.m1, "m1"), 16, (T.off1, "off1"), T.b1, T.win2, [])
+    step(2, T.win2, (T.w2p, "w2p"), (T.w2e, "w2e"), ready, T.x2, T.s2, T.u2, T.ps2, "d2", lambda: None)
+    op("v", "m2", ["sel2", "reset"], v.tensor_tensor_scan, out=T.m2[:], data0=T.reset[:], data1=T.ps2[:, 0:128], initial=0.0,
+       op0=A.add, op1=A.min)
+    ready = spread(3, (T.m2, "m2"), 128, (T.off8, "off8"), T.b2, T.win3, ready)
+    step(3, T.win3, (T.w2p, "w2p"), (T.w2e, "w2e"), ready, T.x3, T.s3, T.u3, T.ps3, "d2", lambda: None)
+    op("v", "m3", ["sel3"], v.tensor_tensor_scan, out=T.m3[:], data0=T.reset[:], data1=T.ps3[:, 0:128], initial=0.0,
+       op0=A.add, op1=A.min)
+    op("v", "yt", ["m3"], v.tensor_copy, out=T.ytile[:], in_=T.m3[:, 7:128:8])
+    op("v", "yown", ["m3"], v.tensor_copy, out=T.landy[:, og:og + 16], in_=T.m3[:, 7:128:8])
+
+    send("yf", ["yt"], [(hs[i], T.hy[:], T.ytile[:], allr[8 * i:8 * i + 8]) for i in range(2)], "hfin", topo, core)
+    send("yn", ["yt"], [(cores[d], T.landy[:, og:og + 16], T.ytile[:], e) for d, e in tod], "aydir", topo, core)
+
+    all_y = ["aydir", "ayrel", "yown"]
+    for j in range(6):
+        op("v", "cl", all_y + ["offy"], v.tensor_scalar, out=T.cl[:, 16 * j:16 * j + 16],
+           in0=T.landy[:, 0:128].indirect(T.offy[:, 0:1]), scalar1=KNOTS[j] * SC, scalar2=-KNOTS[j] * SC, op0=A.min, op1=A.max)
+    op("s", "cl", all_y + ["offy"], s.activation, out=T.cl[:, 96:112], in_=T.landy[:, 0:128].indirect(T.offy[:, 0:1]),
+       func=F.Copy)
+    for j in range(7):
+        op("p", "psy", ["cl", "wid", "own"], p.matmul, out=T.psy[0:16, 0:128], lhsT=T.cl[:, 16 * j:16 * j + 16],
+           rhs=T.wid[:, 128 * j:128 * j + 128], start=j == 0, stop=j == 6)
+    op("v", "eq", all_y + ["own"], v.tensor_tensor, out=T.eq[:], in0=T.landy[:], in1=T.own[:], op=A.is_equal)
+    op("p", "cnt", ["eq", "minef", "minen"], p.matmul, out=T.ps1[0:1, 0:128], lhsT=T.ones[:, 0:1], rhs=T.eq[:], start=True,
+       stop=True)
+    op("s", "yrow", ["psy"], s.activation, out=T.yrow[0:16, :], in_=T.psy[0:16, 0:128], func=F.Copy, bias=float(V // 2))
+    dma("s", "yout", ["yrow"], T.y[:], T.yrow[0:16, :])
+    op("v", "crun", ["cnt", "keep"], v.tensor_tensor_scan, out=T.crun[0:1, :], data0=T.keep[0:1, :], data1=T.ps1[0:1, 0:128],
+       initial=0.0, op0=A.mult, op1=A.add)
+    op("v", "crow", ["crun"], v.tensor_copy, out=T.crow[0:1, :], in_=T.crun[0:1, 15:128:16])
+    dma("y", "cout", ["crow"], T.cnt[:], T.crow[0:1, :])
+    R["finish"]()
+
+
+def send_two(R, T, g, topo, core, name, parts):
+    tr, total = [], 0
+    for jobs, rsem in parts:
+        for dst, out, src, eng in jobs:
+            rid, pid = topo.addr(dst, core)
+            tr.append(RemoteDMATransfer(dst_ids=[DstId(rid=rid, pnc=pid)], dma_engine_mask=sum(1 << e for e in eng),
+                                        remote_sem=T.sem[rsem], src=src, dst=out))
+            total += len(eng)
+    t = R["tag"](name)
+    t["n"] = total
+    g.remote_dma_fused(tr, local_sem=T.sem[t["sem"]])

@@ -1,51 +1,50 @@
+import math
 from concourse.bass import DstId, RemoteDMATransfer
 from concourse.mybir import AluOpType as A, ActivationFunctionType as F
 
 V = 2048
-XA, XB = 768, 1472
-SC = 2.0 ** -15
-BASE = [-16384, -8192, -4096, -2048, -1024, -512, -256, -128, 0, 128, 256, 512, 1024, 2048, 4096, 8192]
-SLOPE = [64, 32, 16, 8, 4, 2, 1, 1, 1, 1, 2, 4, 8, 16, 32, 64]
-KNOTS = [256, 512, 1024, 2048, 4096, 8192]
-WEIGHT = [2.0 ** (14 - j) for j in range(6)] + [2.0 ** 9]
+ROUND = 1.5 * 2.0 ** 18
+CUT1 = (576, 1280, 1792, V)
+CUT = (736, 1376, 1824, V)
+LAST = (("v", 0, 512), ("s", 1024, 1536), ("v", 512, 896), ("s", 1536, 1920), ("v", 896, 1024), ("s", 1920, 2048))
+ROWS = (("s", 0, 3, "pa0"), ("v", 3, 7, "pr0"), ("s", 7, 9, "pa1"), ("v", 9, 13, "pr1"), ("s", 13, 14, "pa2"), ("v", 14, 16, "pr2"))
+BACK = {"a": (0, 4, "pa0", "pr0"), "b": (4, 7, "pa1", "pr1"), "c": (7, 10, "pa2", "pr2"), "d": (10, 13, "pa0", "pr0"),
+        "e": (13, 16, "pa1", "pr1")}
+BACK_ORDER = {"v": "ga mb ma ge mc ca md me cd ce", "s": "gb gc gd cb cc", "p": "sb sa rb sc ra se sd rc rd re"}
 
+bf, f4, i4, u2 = "bfloat16", "float32", "int32", "uint16"
 SCRATCH = {
-    "pmi": ("sbuf", [128, 128], "int32"), "eni": ("sbuf", [128, 128], "int32"),
-    "w1p": ("sbuf", [128, 128], "uint16"), "w1e": ("sbuf", [128, 128], "uint16"),
-    "w2p": ("sbuf", [128, 128], "uint16"), "w2e": ("sbuf", [128, 128], "uint16"),
-    "p2i": ("sbuf", [128, 128], "int32"), "e2i": ("sbuf", [128, 128], "int32"),
-    "first": ("sbuf", [128, V], "bfloat16"),
-    "base": ("sbuf", [128, 128], "bfloat16"), "ones": ("sbuf", [128, 128], "bfloat16"),
-    "ident": ("sbuf", [128, 128], "bfloat16"), "pick": ("sbuf", [128, 8], "bfloat16"),
-    "reset": ("sbuf", [128, 128], "bfloat16"), "keep": ("sbuf", [128, 128], "bfloat16"),
-    "wid": ("sbuf", [128, 7 * 128], "bfloat16"), "own": ("sbuf", [128, 128], "bfloat16"),
-    "pint": ("sbuf", [128, 16], "int32"), "pmod": ("sbuf", [128, 16], "int32"), "phalf": ("sbuf", [128, 16], "int32"),
-    "podd": ("sbuf", [128, 16], "int32"), "psum2": ("sbuf", [128, 16], "int32"),
-    "off1": ("sbuf", [128, 10], "uint16"), "off8": ("sbuf", [128, 10], "uint16"), "offy": ("sbuf", [128, 2], "uint16"),
-    "win1": ("sbuf", [128, V], "bfloat16"), "win2": ("sbuf", [128, V], "bfloat16"), "win3": ("sbuf", [128, V], "bfloat16"),
-    "x1": ("sbuf", [128, V], "bfloat16"), "x2": ("sbuf", [128, V], "bfloat16"), "x3": ("sbuf", [128, V], "bfloat16"),
-    "s1": ("sbuf", [128, V], "bfloat16"), "s2": ("sbuf", [128, V], "bfloat16"), "s3": ("sbuf", [128, V], "bfloat16"),
-    "u1": ("sbuf", [128, V], "bfloat16"), "u2": ("sbuf", [128, V], "bfloat16"), "u3": ("sbuf", [128, V], "bfloat16"),
-    "mine": ("sbuf", [128, 128], "bfloat16"), "landd": ("sbuf", [128, 48], "bfloat16"), "landr": ("sbuf", [128, 64], "bfloat16"),
-    "ea": ("sbuf", [128, 32], "bfloat16"), "ra": ("sbuf", [128, 32], "bfloat16"), "rb": ("sbuf", [128, 32], "bfloat16"),
-    "m1": ("sbuf", [128, 16], "bfloat16"), "m2": ("sbuf", [128, 128], "bfloat16"), "m3": ("sbuf", [128, 128], "bfloat16"),
-    "b1": ("sbuf", [128, 144], "bfloat16"), "b2": ("sbuf", [128, 144], "bfloat16"),
-    "ytile": ("sbuf", [128, 16], "bfloat16"), "landy": ("sbuf", [128, 128], "bfloat16"),
-    "cl": ("sbuf", [128, 7 * 16], "bfloat16"), "eq": ("sbuf", [128, 128], "bfloat16"),
-    "yrow": ("sbuf", [128, 128], "float32"), "crun": ("sbuf", [128, 128], "float32"), "crow": ("sbuf", [128, 8], "float32"),
-    "hu": ("sbuf", [128, 32], "bfloat16"), "hy": ("sbuf", [128, 16], "bfloat16"),
-    "lp": ("dram", [8, 128, 16], "int32"), "le": ("dram", [8, 128, 16], "int32"), "ls": ("dram", [8, 128, 16], "int32"),
-    "dp": ("dram", [8, 128, 16], "int32"), "de": ("dram", [8, 128, 16], "int32"), "ds": ("dram", [8, 128, 16], "int32"),
-    "hp": ("dram", [2, 128, 16], "int32"), "he": ("dram", [2, 128, 16], "int32"), "hs": ("dram", [2, 128, 16], "int32"),
-    "psb": ("psum", [128, V], "float32"),
-    "ps1": ("psum", [128, 512], "float32"), "ps2": ("psum", [128, 512], "float32"), "ps3": ("psum", [128, 512], "float32"),
-    "psy": ("psum", [128, 512], "float32"),
+    "pmi": ("sbuf", [128, 128], i4), "eni": ("sbuf", [128, 128], i4), "sti": ("sbuf", [128, 128], i4),
+    "p2i": ("sbuf", [128, 128], i4), "e2i": ("sbuf", [128, 128], i4),
+    "w1p": ("sbuf", [128, 128], u2), "w1e": ("sbuf", [128, 128], u2), "w2p": ("sbuf", [128, 128], u2), "w2e": ("sbuf", [128, 128], u2),
+    "stb": ("sbuf", [128, 128], bf),
+    "ratio": ("sbuf", [128, 128], f4), "base": ("sbuf", [128, 128], bf), "ones": ("sbuf", [128, 128], bf),
+    "ident": ("sbuf", [128, 128], bf), "pick": ("sbuf", [128, 16], bf), "id32": ("sbuf", [128, 128], "float16"),
+    "reset": ("sbuf", [128, 256], bf), "keep": ("sbuf", [128, 64], bf), "own": ("sbuf", [128, 128], bf),
+    "pint": ("sbuf", [128, 16], i4), "pmod": ("sbuf", [128, 16], i4), "off1": ("sbuf", [128, 10], u2),
+    "win1": ("sbuf", [128, V], bf), "win2": ("sbuf", [128, V], bf), "win3": ("sbuf", [128, V], bf),
+    "xu1": ("sbuf", [128, 2 * V], bf), "x2": ("sbuf", [128, V], bf), "x3": ("sbuf", [128, V], bf),
+    "s1": ("sbuf", [128, V], bf), "s2": ("sbuf", [128, V], bf), "s3": ("sbuf", [128, V], bf),
+    "u2": ("sbuf", [128, V], bf), "u3": ("sbuf", [128, V], bf),
+    "mine": ("sbuf", [128, 288], bf), "land": ("sbuf", [128, 288], bf),
+    "ea": ("sbuf", [128, 32], bf), "eb": ("sbuf", [128, 16], bf), "erep": ("sbuf", [128, 144], bf),
+    "ra": ("sbuf", [128, 32], bf), "rb": ("sbuf", [128, 16], bf), "b1": ("sbuf", [128, 144], bf),
+    "m3": ("sbuf", [128, 128], bf), "ytile": ("sbuf", [128, 16], bf), "landy": ("sbuf", [128, 128], bf),
+    "lg": ("sbuf", [128, 16], f4), "dec": ("sbuf", [128, 16], "float16"), "eq": ("sbuf", [128, 128], bf),
+    "yrow": ("sbuf", [128, 128], f4), "crun": ("sbuf", [128, 128], f4), "crow": ("sbuf", [128, 8], f4),
+    "hu": ("sbuf", [128, 64], bf), "hy": ("sbuf", [128, 16], bf),
+    "lp": ("dram", [8, 128, 16], i4), "le": ("dram", [8, 128, 16], i4),
+    "dp": ("dram", [8, 128, 16], i4), "de": ("dram", [8, 128, 16], i4),
+    "hp": ("dram", [2, 128, 16], i4), "he": ("dram", [2, 128, 16], i4),
+    "first": ("psum", [128, V], bf),
+    "pa0": ("psum", [128, 512], f4), "pa1": ("psum", [128, 512], f4), "pa2": ("psum", [128, 512], f4),
+    "pr0": ("psum", [128, 1024], bf), "pr1": ("psum", [128, 1024], bf), "pr2": ("psum", [128, 1024], bf),
 }
-NT = 128
-SEMAPHORES = ["t%d" % i for i in range(NT)] + ["alist", "astart", "adir", "arel", "aydir", "ayrel", "hlist", "hstart", "hlab", "hfin"]
+NT = 138
+SEMAPHORES = ["t%d" % i for i in range(NT)] + ["alist", "adir", "arel", "aydir", "ayrel", "hlist", "hlab", "hfin"]
 
 
-def runner(g, T):
+def runner(g, T, topo, core):
     Q = {"g": g, "v": g.vector, "s": g.scalar, "p": g.tensor, "y": g.sync}
     tags, know, count = {}, {k: set() for k in Q}, [0]
 
@@ -73,15 +72,21 @@ def runner(g, T):
         t["know"] |= know[q]
         return T.sem[t["sem"]]
 
-    def op(q, name, after, call, n=1, **kw):
+    def op(q, name, after, call, **kw):
         wait(q, after)
-        call(**kw).then_inc(raised(q, name, n), n)
+        call(**kw).then_inc(raised(q, name, 1), 1)
+
+    def copy(q, name, after, out, in_):
+        if q == "v":
+            op(q, name, after, g.vector.tensor_copy, out=out, in_=in_)
+        else:
+            op(q, name, after, g.scalar.activation, out=out, in_=in_, func=F.Copy)
 
     def dma(q, name, after, out, in_):
         wait(q, after)
         Q[q].dma_start(out=out, in_=in_).then_inc(raised(q, name, 16), 16)
 
-    def send(name, after, jobs, rsem, topo, core):
+    def send(name, after, jobs, rsem):
         wait("g", after)
         tr, total = [], 0
         for dst, out, src, eng in jobs:
@@ -94,7 +99,7 @@ def runner(g, T):
     def finish():
         wait("g", [a for a in tags if not tags[a]["waited"]])
 
-    return {"tag": tag, "wait": wait, "op": op, "dma": dma, "send": send, "finish": finish}
+    return tag, op, copy, dma, send, finish
 
 
 def plan(T, topo):
@@ -112,31 +117,34 @@ def helpers(T, topo, q, far):
             and all(topo.may_write(h, T.cores[d]) for d in far)][:2]
 
 
-def helper_program(g, core, T, topo, q, far, mine):
-    r = runner(g, T)
+def helper_program(g, core, T, topo, q, mine):
+    tag, op, copy, dma, send, finish = runner(g, T, topo, core)
     cores, near, owners, group = plan(T, topo)
     dst = [cores[d] for d in mine]
     e = topo.engines(core, dst[0])
-    slot = near[mine[0]]
-    fr = [p for p in range(len(cores)) if p not in slot]
-    s = fr.index(q)
-    h = len(e) // 2
-    k = len(e) // 4
-    r["tag"]("hlist", "hlist", 4)
-    r["tag"]("hstart", "hstart", 4)
-    r["tag"]("hlab", "hlab", 8)
-    r["tag"]("hfin", "hfin", 8)
+    h, gq = len(e) // 2, group[q]
+    tag("hlist", "hlist", 8)
+    tag("hlab", "hlab", 8)
+    tag("hfin", "hfin", 8)
     jobs = []
     for i in range(2):
-        jobs.append((dst[i], T.dp[q], T.hp[i], e[2 * i * k:(2 * i + 1) * k]))
-        jobs.append((dst[i], T.de[q], T.he[i], e[(2 * i + 1) * k:(2 * i + 2) * k]))
-    r["send"]("fl", ["hlist"], jobs, "alist", topo, core)
-    r["send"]("fs", ["hstart"], [(dst[i], T.ds[q], T.hs[i], e[h * i:h * i + h]) for i in range(2)], "astart", topo, core)
-    r["send"]("fu", ["hlab"], [(dst[i], T.landr[:, 16 * s:16 * s + 16], T.hu[:, 16 * i:16 * i + 16], e[h * i:h * i + h])
-                               for i in range(2)], "arel", topo, core)
-    r["send"]("fy", ["hfin"], [(dst[i], T.landy[:, 16 * group[q]:16 * group[q] + 16], T.hy[:], e[h * i:h * i + h])
-                               for i in range(2)], "ayrel", topo, core)
-    r["finish"]()
+        k = e[h * i:h * i + h]
+        jobs += [(dst[i], T.dp[gq], T.hp[i], k[0:2]), (dst[i], T.de[gq], T.he[i], k[2:4])]
+    send("fl", ["hlist"], jobs, "alist")
+    send("fu", ["hlab"], [(dst[i], T.land[:, 32 * gq:32 * gq + 32], T.hu[:, 32 * i:32 * i + 32], e[h * i:h * i + h])
+                          for i in range(2)], "arel")
+    send("fy", ["hfin"], [(dst[i], T.landy[:, 16 * gq:16 * gq + 16], T.hy[:], e[h * i:h * i + h]) for i in range(2)], "ayrel")
+    finish()
+
+
+def weave(orders, needs, emit):
+    left = {q: o.split() for q, o in orders.items()}
+    done = set()
+    while any(left.values()):
+        q = [q for q in left if left[q] and all(n in done for n in needs(left[q][0]))][0]
+        name = left[q].pop(0)
+        emit(q, name)
+        done.add(name)
 
 
 def rank_program(g, core, T, topo):
@@ -149,10 +157,9 @@ def rank_program(g, core, T, topo):
                 hs = helpers(T, topo, q, far)
                 if core in hs:
                     i = hs.index(core)
-                    helper_program(g, core, T, topo, q, far, far[2 * i:2 * i + 2])
+                    helper_program(g, core, T, topo, q, far[2 * i:2 * i + 2])
         return
-    R = runner(g, T)
-    op, dma, send, tag, wait = R["op"], R["dma"], R["send"], R["tag"], R["wait"]
+    tag, op, copy, dma, send, finish = runner(g, T, topo, core)
     v, s, p = g.vector, g.scalar, g.tensor
     go = group[rank]
     far = [d for d in owners if d not in near[rank]]
@@ -162,188 +169,196 @@ def rank_program(g, core, T, topo):
     off = topo.engines(core, cores[plane[0]])
     allr = topo.engines(core, hs[0])
     on = [x for x in allr if x not in off]
-    for nm, n in (("alist", 24), ("astart", 24), ("adir", 16), ("arel", 16), ("aydir", 16), ("ayrel", 16)):
+    tod = [(mate, on), (plane[0], off[0:4]), (plane[1], off[4:8])]
+    for nm, n in (("alist", 32), ("adir", 16), ("arel", 16), ("aydir", 16), ("ayrel", 16)):
         tag(nm, nm, n)
 
-    def slot(d):
-        return [x for x in near[d] if x != d].index(rank)
-
     dma("y", "pm", [], T.pmi[:], T.pm[:])
+    dma("s", "st", [], T.sti[:], T.st[:])
+    dma("y", "lists", [], T.lp[:], T.pm[:])
     dma("s", "en", [], T.eni[:], T.en[:])
-    dma("y", "lpe", [], T.lp[:], T.pm[:])
-    dma("s", "lpe", [], T.le[:], T.en[:])
-    dma("y", "ls", [], T.ls[:], T.st[:])
-    dma("y", "ownl", [], T.dp[rank], T.pm[16 * go:16 * go + 16, :])
-    dma("y", "ownl", [], T.de[rank], T.en[16 * go:16 * go + 16, :])
-    dma("y", "owns", [], T.ds[rank], T.st[go:go + 1, :])
+    dma("y", "lists", [], T.le[:], T.en[:])
+    dma("y", "ownl", [], T.dp[go], T.pm[16 * go:16 * go + 16, :])
+    dma("y", "ownl", [], T.de[go], T.en[16 * go:16 * go + 16, :])
 
-    op("g", "base", [], g.iota, out=T.base[:], pattern=[[1, 128]], base=0, channel_multiplier=0,
-       allow_small_or_imprecise_dtypes=True)
-    op("v", "mfirst", [], v.memset, ap=T.first[:], constant=0.0)
     op("v", "ones", [], v.memset, ap=T.ones[:], constant=1.0)
-    wait("g", ["mfirst"])
-    dma("g", "d1", ["mfirst"], T.first[0:128:16, :], T.st[:])
-    for i in range(16):
-        o = T.win1[:, 128 * i:128 * i + 128]
-        if i % 8 < 5:
-            op("v", "win1", ["base"], v.tensor_scalar, out=o, in0=T.base[:], scalar1=SLOPE[i] * SC, scalar2=BASE[i] * SC,
-               op0=A.mult, op1=A.add)
-        else:
-            op("s", "win1", ["base"], s.activation, out=o, in_=T.base[:], func=F.Identity, scale=SLOPE[i] * SC, bias=0.0) \
-                if BASE[i] == 0 else op("s", "win1", ["base"], s.activation, out=o, in_=T.base[:], func=F.Copy,
-                                        scale=SLOPE[i] * SC, bias=BASE[i] * SC)
-    op("g", "pick", ["ones"], g.affine_select, out=T.pick[:], in_=T.ones[:, 0:8], pattern=[[-16, 8]], compare_op=A.is_equal,
-       fill=0.0, base=0, channel_multiplier=1)
-    jobs = []
-    for i, d in enumerate(far):
-        jobs.append((hs[i // 2], T.hp[i % 2], T.lp[group[d]], [on[2 * i]]))
-        jobs.append((hs[i // 2], T.he[i % 2], T.le[group[d]], [on[2 * i + 1]]))
-    direct = [(plane[0], off[0:1], off[1:2]), (plane[1], off[2:3], off[3:4]), (mate, off[4:6], off[6:8])]
-    toh = jobs
-    tod = []
-    for d, ea, eb in direct:
-        tod.append((cores[d], T.dp[rank], T.lp[group[d]], ea))
-        tod.append((cores[d], T.de[rank], T.le[group[d]], eb))
-    wait("g", ["lpe"])
-    send_two(R, T, g, topo, core, "cl1", [(toh, "hlist"), (tod, "alist")])
-    wait("g", ["ls"])
-    toh = [(hs[i // 2], T.hs[i % 2], T.ls[group[d]], on[2 * i:2 * i + 2]) for i, d in enumerate(far)]
-    tod = [(cores[d], T.ds[rank], T.ls[group[d]], ea + eb) for d, ea, eb in direct]
-    send_two(R, T, g, topo, core, "cl2", [(toh, "hstart"), (tod, "astart")])
-
-    def step(h, win, wp, we, ready, x, sc, u, ps, first, extra):
-        n = lambda t: t + str(h)
-        op("v", n("ga"), ready + [wp[1]], v.tensor_copy, out=x[:, 0:XA], in_=win[:, 0:V].indirect(wp[0][:, 0:XA // 16]))
-        op("s", n("gb"), ready + [wp[1]], s.activation, out=x[:, XA:XB], in_=win[:, 0:V].indirect(wp[0][:, XA // 16:XB // 16]),
-           func=F.Copy)
-        op("s", n("gc"), ready, s.activation, out=x[:, XB:V], in_=win[:, 0:V].indirect(wp[0][:, XB // 16:V // 16]), func=F.Copy)
-        extra()
-        last = None
-        for a, b, t in ((0, XA, "ga"), (XA, XB, "gb"), (XB, V, "gc")):
-            op("v", n("sc" + t), [n(t), first] + ([last] if last else []), v.tensor_tensor_scan, out=sc[:, a:b],
-               data0=T.first[:, a:b], data1=x[:, a:b], initial=0.0 if a == 0 else sc[:, a - 1:a], op0=A.add, op1=A.min)
-            last = n("sc" + t)
-        parts = (("v", 0, 768), ("s", 1024, 1792), ("v", 768, 1024), ("s", 1792, 2048))
-        for q, a, b in parts:
-            o, i_ = u[:, a:b], sc[:, 0:V].indirect(we[0][:, a // 16:b // 16])
-            if q == "v":
-                op("v", n("u%d" % a), [last, we[1]], v.tensor_copy, out=o, in_=i_)
-            else:
-                op("s", n("u%d" % a), [last, we[1]], s.activation, out=o, in_=i_, func=F.Copy)
-        for q, a, b in parts:
-            for i in range(a // 128, b // 128):
-                o = ps[:, i:128:16] if h == 1 else ps[:, 8 * i:8 * i + 8]
-                op("p", n("sel"), [n("u%d" % a), "pick"], p.matmul, out=o, lhsT=u[:, 128 * i:128 * i + 128], rhs=T.pick[:],
-                   start=True, stop=True)
-
-    op("v", "w1p", ["pm"], v.tensor_copy, out=T.w1p[:], in_=T.pmi[:])
-    step(1, T.win1, (T.w1p, "w1p"), (T.w1e, "w1e"), ["win1"], T.x1, T.s1, T.u1, T.ps1, "d1",
-         lambda: op("v", "w1e", ["en"], v.tensor_copy, out=T.w1e[:], in_=T.eni[:]))
-    fa = 16 * group[far[0]]
-    na = 64 - fa
-    op("v", "minef", ["sel1"], v.tensor_copy, out=T.mine[:, fa:fa + 64], in_=T.ps1[:, fa:fa + 64])
-    op("v", "minen", ["sel1"], v.tensor_copy, out=T.mine[:, na:na + 64], in_=T.ps1[:, na:na + 64])
-    send("sf", ["minef"], [(hs[i], T.hu[:], T.mine[:, fa + 32 * i:fa + 32 * i + 32], allr[8 * i:8 * i + 8]) for i in range(2)],
-         "hlab", topo, core)
-    tod = [(mate, on), (plane[0], off[0:4]), (plane[1], off[4:8])]
-    send("sn", ["minen"], [(cores[d], T.landd[:, 16 * slot(d):16 * slot(d) + 16],
-                            T.mine[:, 16 * group[d]:16 * group[d] + 16], e) for d, e in tod], "adir", topo, core)
-    dma("g", "d2", ["astart", "owns", "scgc1"], T.first[0:128:16, :], T.ds[:])
+    op("v", "ratio", [], v.memset, ap=T.ratio[:], constant=math.exp(1 / 32))
+    op("v", "base", ["ones", "ratio"], v.tensor_tensor_scan, out=T.base[:], data0=T.ratio[:], data1=T.ones[:],
+       initial=math.exp(-129 / 32), op0=A.mult, op1=A.mult)
     op("g", "ident", ["ones"], g.affine_select, out=T.ident[:], in_=T.ones[:], pattern=[[-1, 128]], compare_op=A.is_equal,
        fill=0.0, base=0, channel_multiplier=1)
-    op("g", "reset", ["ones"], g.affine_select, out=T.reset[:], in_=T.ones[:], pattern=[[0, 16], [1, 8]],
-       compare_op=A.is_equal, fill=0.0, base=0, channel_multiplier=0)
+    op("g", "pick", [], g.affine_select, out=T.pick[:], in_=T.ones[:, 0:16], pattern=[[0, 2], [-16, 8]],
+       compare_op=A.is_equal, fill=0.0, base=0, channel_multiplier=1)
     op("g", "pint", [], g.iota, out=T.pint[:], pattern=[[0, 16]], base=0, channel_multiplier=1)
+    op("v", "zpad", [], v.memset, ap=T.mine[:], constant=0.0)
+    op("v", "lpad", [], v.memset, ap=T.land[:, 256:288], constant=0.0)
+    for i in range(16):
+        o, c = T.win1[:, 128 * i:128 * i + 128], math.exp(4.0 * (i - 15))
+        if i % 8 < 5:
+            op("v", "win1", ["base"], v.tensor_scalar, out=o, in0=T.base[:], scalar1=c, scalar2=None, op0=A.mult)
+        else:
+            op("s", "win1", ["base"], s.activation, out=o, in_=T.base[:], func=F.Copy, scale=c)
+
+    two = ((T.hp, T.dp, T.lp), (T.he, T.de, T.le))
+    send("cl1", ["lists"], [(hs[i // 2], h[i % 2], l[group[d]], allr[8 * k + 2 * i:8 * k + 2 * i + 2])
+                            for k, (h, dd, l) in enumerate(two) for i, d in enumerate(far)], "hlist")
+    send("cl2", [], [(cores[d], dd[go], l[group[d]], e[len(e) // 2 * k:len(e) // 2 * (k + 1)])
+                     for k, (h, dd, l) in enumerate(two) for d, e in tod], "alist")
+
+    def starts(h, src, after):
+        for i in range(16):
+            op("p", ("fa%d" if i < 8 else "fb%d") % h, after, p.transpose, out=T.first[:, 128 * i:128 * i + 128],
+               in_=src[:, 2 * i + 1:2 * i + 257:2], identity=T.ident[:])
+
+    def own_starts():
+        copy("v", "stb", ["st"], T.stb[:], T.sti[:])
+        op("p", "stt", ["stb", "ident"], p.transpose, out=T.pr0[:, 0:128], in_=T.stb[:], identity=T.ident[:])
+        copy("v", "w1e", ["en"], T.w1e[:], T.eni[:])
+        copy("v", "zs", ["stt", "zpad"], T.mine[:, 1:256:2], T.pr0[:, 0:128])
+        starts(1, T.mine, ["zs"])
+
+    def scatter_scan(h, win, wp, ready, x, sc, cut, first, between=None):
+        n = lambda t: t + str(h)
+        cuts = list(zip((0,) + cut[:-1], cut))
+        for k, (a, b) in enumerate(cuts):
+            if k:
+                copy("s", n("x%d" % k), ready + [wp[1]], x[:, a:b], win[:, 0:V].indirect(wp[0][:, a // 16:b // 16]))
+        if between:
+            between()
+        copy("v", n("x0"), ready + [wp[1]], x[:, 0:cut[0]], win[:, 0:V].indirect(wp[0][:, 0:cut[0] // 16]))
+        for k, (a, b) in enumerate(cuts):
+            op("v", n("sc%d" % k), [n("x%d" % k)] + first[:2 if k else 1] + ([n("sc%d" % (k - 1))] if k else []),
+               v.tensor_tensor_scan, out=sc[:, a:b], data0=T.first[:, a:b], data1=x[:, a:b],
+               initial=sc[:, a - 1:a] if k else 0.0, op0=A.add, op1=A.min)
+        return n("sc%d" % (len(cuts) - 1))
+
+    def columns(h, sc, we, last, u, at, ps):
+        for q, a, b in LAST:
+            copy(q, "u%d_%d" % (h, a), [last, we[1]], u[:, at + a:at + b], sc[:, 0:V].indirect(we[0][:, a // 16:b // 16]))
+        for q, a, b in LAST:
+            for i in range(a // 128, b // 128):
+                op("p", "sel%d" % h, ["u%d_%d" % (h, a), "pick"], p.matmul,
+                   out=ps[:, i:128:16] if h == 1 else ps[:, 8 * i:8 * i + 8],
+                   lhsT=u[:, at + 128 * i:at + 128 * i + 128], rhs=T.pick[:, 0:8], start=True, stop=True)
+
+    copy("v", "w1p", ["pm"], T.w1p[:], T.pmi[:])
+    last = scatter_scan(1, T.win1, (T.w1p, "w1p"), ["win1"], T.xu1, T.s1, CUT1, ["fa1", "fb1"], own_starts)
+    columns(1, T.s1, (T.w1e, "w1e"), last, T.xu1, V, T.pa0)
+    fa = 16 * group[far[0]]
+    na = 64 - fa
+    og = 16 * go
+    copy("v", "minef", ["sel1"], T.mine[:, 2 * fa:2 * fa + 128:2], T.pa0[:, fa:fa + 64])
+    copy("v", "minen", ["sel1"], T.mine[:, 2 * na:2 * na + 128:2], T.pa0[:, na:na + 64])
+    send("sf", ["minef"], [(hs[i], T.hu[:], T.mine[:, 2 * fa + 64 * i:2 * fa + 64 * i + 64], allr[8 * i:8 * i + 8])
+                           for i in range(2)], "hlab")
+    send("sn", ["minen"], [(cores[d], T.land[:, 2 * og:2 * og + 32], T.mine[:, 32 * group[d]:32 * group[d] + 32], e)
+                           for d, e in tod], "adir")
+    copy("v", "lown", ["minen"], T.land[:, 2 * og:2 * og + 32], T.mine[:, 2 * og:2 * og + 32])
 
     dma("y", "p2i", ["alist", "ownl"], T.p2i[:], T.dp[:])
-    dma("y", "e2i", ["alist", "ownl"], T.e2i[:], T.de[:])
+    dma("y", "e2i", [], T.e2i[:], T.de[:])
     op("v", "pmod", ["pint"], v.tensor_scalar, out=T.pmod[:], in0=T.pint[:], scalar1=15, scalar2=None, op0=A.bitwise_and)
-    op("v", "off1", ["pmod"], v.tensor_scalar, out=T.off1[:], in0=T.pmod[:, 0:10], scalar1=1, scalar2=None, op0=A.mult)
-    op("v", "off8", ["pmod"], v.tensor_scalar, out=T.off8[:], in0=T.pmod[:, 0:10], scalar1=8, scalar2=7, op0=A.mult, op1=A.add)
-    op("v", "podd", ["pmod"], v.tensor_scalar, out=T.podd[:], in0=T.pmod[:], scalar1=1, scalar2=None, op0=A.bitwise_and)
-    op("v", "phalf", ["podd"], v.tensor_scalar, out=T.phalf[:], in0=T.pmod[:], scalar1=8, scalar2=2 * rank, op0=A.mult,
-       op1=A.add)
-    op("v", "podd7", ["podd"], v.tensor_scalar, out=T.psum2[:], in0=T.podd[:], scalar1=7, scalar2=None, op0=A.mult)
-    op("v", "podd8", ["podd7", "phalf"], v.tensor_tensor, out=T.podd[:], in0=T.phalf[:], in1=T.psum2[:], op=A.subtract)
-    op("v", "offy", ["podd8"], v.tensor_scalar, out=T.offy[:], in0=T.podd[:, 0:2], scalar1=1, scalar2=None, op0=A.mult)
+    op("v", "reset0", [], v.memset, ap=T.reset[:], constant=0.0)
     op("v", "keep0", [], v.memset, ap=T.keep[:], constant=1.0)
-    op("v", "keep", ["keep0"], v.memset, ap=T.keep[:, 0:128:16], constant=0.0)
-    for j in range(7):
-        op("s", "wid", ["ident"], s.activation, out=T.wid[:, 128 * j:128 * j + 128], in_=T.ident[:], func=F.Copy,
-           scale=WEIGHT[j])
+    op("v", "id32", [], v.tensor_scalar, out=T.id32[:], in0=T.ident[:], scalar1=32.0, scalar2=None, op0=A.mult)
+    op("v", "off1", ["pmod"], v.tensor_scalar, out=T.off1[:], in0=T.pmod[:, 0:10], scalar1=1, scalar2=None, op0=A.mult)
+    op("v", "reset", ["reset0"], v.memset, ap=T.reset[:, 0:256:16], constant=1.0)
+    op("v", "keep", ["keep0"], v.memset, ap=T.keep[:, 0:64:16], constant=0.0)
     for i in range(16):
-        op("p", "qown", ["win1", "pick"], p.matmul, out=T.psy[:, i:128:16], lhsT=T.win1[:, 128 * i:128 * i + 128],
-           rhs=T.pick[:], start=True, stop=True)
-    op("s", "own", ["qown"], s.activation, out=T.own[:], in_=T.psy[:, 0:128], func=F.Copy)
-    op("v", "w2p", ["p2i"], v.tensor_copy, out=T.w2p[:], in_=T.p2i[:])
-    op("v", "w2e", ["e2i"], v.tensor_copy, out=T.w2e[:], in_=T.e2i[:])
+        op("p", "qown", [], p.matmul, out=T.pa1[:, i:128:16], lhsT=T.win1[:, 128 * i:128 * i + 128],
+           rhs=T.pick[:, 0:8], start=True, stop=True)
+    copy("s", "own", ["qown"], T.own[:], T.pa1[:, 0:128])
 
-    og = 16 * go
-    op("v", "ea", ["adir"], v.tensor_tensor, out=T.ea[:, 0:16], in0=T.landd[:, 0:16], in1=T.landd[:, 16:32], op=A.min)
-    op("v", "ea", ["minen"], v.tensor_tensor, out=T.ea[:, 16:32], in0=T.landd[:, 32:48], in1=T.mine[:, og:og + 16], op=A.min)
-    op("v", "ra", ["arel"], v.tensor_tensor, out=T.ra[:], in0=T.landr[:, 0:32], in1=T.landr[:, 32:64], op=A.min)
-    op("v", "rb", ["ra", "ea"], v.tensor_tensor, out=T.rb[:], in0=T.ra[:], in1=T.ea[:], op=A.min)
-    op("v", "m1", ["rb"], v.tensor_tensor, out=T.m1[:], in0=T.rb[:, 0:16], in1=T.rb[:, 16:32], op=A.min)
-
-    def spread(h, src, n, offs, b, win, free):
-        op("v", "rep%d" % h, [src[1], offs[1]], v.tensor_copy, out=b[:], in_=src[0][:, 0:n].indirect(offs[0][:, 0:9]))
-        out = []
-        for k in range(4):
-            for i in range(4 * k, 4 * k + 4):
-                op("p", "row%d%d" % (h, k), ["rep%d" % h, "ident"] + free, p.matmul, out=T.psb[:, 128 * i:128 * i + 128],
-                   lhsT=b[:, i:i + 128], rhs=T.ident[:], start=True, stop=True)
-            o, i_ = win[:, 512 * k:512 * k + 512], T.psb[:, 512 * k:512 * k + 512]
-            t = "w%d%d" % (h, k)
-            if k % 2:
-                op("v", t, ["row%d%d" % (h, k)], v.tensor_copy, out=o, in_=i_)
+    op("v", "ea", ["adir", "lown"], v.tensor_tensor, out=T.ea[:], in0=T.land[:, 2 * na:2 * na + 64:2],
+       in1=T.land[:, 2 * na + 64:2 * na + 128:2], op=A.min)
+    op("v", "eb", ["ea"], v.tensor_tensor, out=T.eb[:], in0=T.ea[:, 0:16], in1=T.ea[:, 16:32], op=A.min)
+    copy("v", "erep", ["eb", "off1"], T.erep[:], T.eb[:, 0:16].indirect(T.off1[:, 0:9]))
+    op("v", "ra", ["arel"], v.tensor_tensor, out=T.ra[:], in0=T.land[:, 2 * fa:2 * fa + 64:2],
+       in1=T.land[:, 2 * fa + 64:2 * fa + 128:2], op=A.min)
+    op("v", "rb", ["ra"], v.tensor_tensor, out=T.rb[:], in0=T.ra[:, 0:16], in1=T.ra[:, 16:32], op=A.min)
+    op("v", "b1", ["rb", "erep"], v.tensor_tensor, out=T.b1[:], in0=T.rb[:, 0:16].indirect(T.off1[:, 0:9]), in1=T.erep[:],
+       op=A.min)
+    copy("v", "w2p", ["p2i"], T.w2p[:], T.p2i[:])
+    copy("v", "w2e", ["e2i"], T.w2e[:], T.e2i[:])
+    for q, a, b, ps in ROWS:
+        for i in range(a, b):
+            o, l = T[ps][:, 128 * (i - a):128 * (i - a + 1)], T.b1[:, i:i + 128]
+            if q == "v":
+                op("p", "row%d" % a, ["b1"], p.transpose, out=o, in_=l, identity=T.ident[:])
             else:
-                op("s", t, ["row%d%d" % (h, k)], s.activation, out=o, in_=i_, func=F.Copy)
-            out.append(t)
-        return out
+                op("p", "row%d" % a, ["b1", "own"], p.matmul, out=o, lhsT=l, rhs=T.ident[:], start=True, stop=True)
+        copy(q, "win2", ["row%d" % a], T.win2[:, 128 * a:128 * b], T[ps][:, 0:128 * (b - a)])
+    starts(2, T.land, ["lpad"])
 
-    ready = spread(2, (T.m1, "m1"), 16, (T.off1, "off1"), T.b1, T.win2, [])
-    step(2, T.win2, (T.w2p, "w2p"), (T.w2e, "w2e"), ready, T.x2, T.s2, T.u2, T.ps2, "d2", lambda: None)
-    op("v", "m2", ["sel2", "reset"], v.tensor_tensor_scan, out=T.m2[:], data0=T.reset[:], data1=T.ps2[:, 0:128], initial=0.0,
+    last = scatter_scan(2, T.win2, (T.w2p, "w2p"), ["win2"], T.x2, T.s2, CUT, ["fa2", "fb2"])
+    names = list(BACK)
+
+    def needs(c):
+        k, x = c[0], c[1]
+        if k == "g":
+            return []
+        bank = {"s": 2, "r": 3}.get(k)
+        prev = [y for y in names[:names.index(x)] if bank and BACK[y][bank] == BACK[x][bank]]
+        return [{"s": "g", "m": "s", "r": "m", "c": "r"}[k] + x] + [{"s": "m", "r": "c"}[k] + y for y in prev]
+
+    def emit(q, c):
+        k, x = c[0], c[1]
+        a, b, pa, pr = BACK[x]
+        after = ["bk" + n for n in needs(c)]
+        if k == "g":
+            copy(q, "bk" + c, [last, "w2e"], T.u2[:, 128 * a:128 * b], T.s2[:, 0:V].indirect(T.w2e[:, 8 * a:8 * b]))
+        elif k == "s":
+            for i in range(a, b):
+                op(q, "bk" + c, after, p.matmul, out=T[pa][:, 16 * (i - a):16 * (i - a + 1)],
+                   lhsT=T.u2[:, 128 * i:128 * i + 128], rhs=T.pick[:], start=True, stop=True)
+        elif k == "m":
+            op(q, "bk" + c, after + ["reset"], v.tensor_tensor_scan, out=T.xu1[:, 256 * a:256 * b:16],
+               data0=T.reset[:, 0:16 * (b - a)], data1=T[pa][:, 0:16 * (b - a)], initial=0.0, op0=A.add, op1=A.min)
+        elif k == "r":
+            for i in range(a, b):
+                op(q, "bk" + c, after, p.transpose, out=T[pr][:, 128 * (i - a):128 * (i - a + 1)],
+                   in_=T.xu1[:, 256 * i + 128:256 * i + 256], identity=T.ident[:])
+        else:
+            copy(q, "bk" + c, after, T.win3[:, 128 * a:128 * b], T[pr][:, 0:128 * (b - a)])
+
+    weave(BACK_ORDER, needs, emit)
+
+    last = scatter_scan(3, T.win3, (T.w2p, "w2p"), ["bkc" + x for x in names], T.x3, T.s3, CUT, ["fa2", "fb2"])
+    columns(3, T.s3, (T.w2e, "w2e"), last, T.u3, 0, T.pa1)
+    op("v", "m3", ["sel3"], v.tensor_tensor_scan, out=T.m3[:], data0=T.reset[:, 0:256:2], data1=T.pa1[:, 0:128], initial=0.0,
        op0=A.add, op1=A.min)
-    ready = spread(3, (T.m2, "m2"), 128, (T.off8, "off8"), T.b2, T.win3, ready)
-    step(3, T.win3, (T.w2p, "w2p"), (T.w2e, "w2e"), ready, T.x3, T.s3, T.u3, T.ps3, "d2", lambda: None)
-    op("v", "m3", ["sel3"], v.tensor_tensor_scan, out=T.m3[:], data0=T.reset[:], data1=T.ps3[:, 0:128], initial=0.0,
-       op0=A.add, op1=A.min)
-    op("v", "yt", ["m3"], v.tensor_copy, out=T.ytile[:], in_=T.m3[:, 7:128:8])
-    op("v", "yown", ["m3"], v.tensor_copy, out=T.landy[:, og:og + 16], in_=T.m3[:, 7:128:8])
+    copy("v", "yt", ["m3"], T.ytile[:], T.m3[:, 7:128:8])
+    copy("v", "yown", ["m3"], T.landy[:, og:og + 16], T.m3[:, 7:128:8])
 
-    send("yf", ["yt"], [(hs[i], T.hy[:], T.ytile[:], allr[8 * i:8 * i + 8]) for i in range(2)], "hfin", topo, core)
-    send("yn", ["yt"], [(cores[d], T.landy[:, og:og + 16], T.ytile[:], e) for d, e in tod], "aydir", topo, core)
+    send("yf", ["yt"], [(hs[i], T.hy[:], T.ytile[:], allr[8 * i:8 * i + 8]) for i in range(2)], "hfin")
+    send("yn", ["yt"], [(cores[d], T.landy[:, og:og + 16], T.ytile[:], e) for d, e in tod], "aydir")
 
-    all_y = ["aydir", "ayrel", "yown"]
-    for j in range(6):
-        op("v", "cl", all_y + ["offy"], v.tensor_scalar, out=T.cl[:, 16 * j:16 * j + 16],
-           in0=T.landy[:, 0:128].indirect(T.offy[:, 0:1]), scalar1=KNOTS[j] * SC, scalar2=-KNOTS[j] * SC, op0=A.min, op1=A.max)
-    op("s", "cl", all_y + ["offy"], s.activation, out=T.cl[:, 96:112], in_=T.landy[:, 0:128].indirect(T.offy[:, 0:1]),
-       func=F.Copy)
-    for j in range(7):
-        op("p", "psy", ["cl", "wid", "own"], p.matmul, out=T.psy[0:16, 0:128], lhsT=T.cl[:, 16 * j:16 * j + 16],
-           rhs=T.wid[:, 128 * j:128 * j + 128], start=j == 0, stop=j == 6)
-    op("v", "eq", all_y + ["own"], v.tensor_tensor, out=T.eq[:], in0=T.landy[:], in1=T.own[:], op=A.is_equal)
-    op("p", "cnt", ["eq", "minef", "minen"], p.matmul, out=T.ps1[0:1, 0:128], lhsT=T.ones[:, 0:1], rhs=T.eq[:], start=True,
-       stop=True)
-    op("s", "yrow", ["psy"], s.activation, out=T.yrow[0:16, :], in_=T.psy[0:16, 0:128], func=F.Copy, bias=float(V // 2))
+    def ln(name, after, out, in_):
+        op("s", name, after, s.activation, out=out, in_=in_, func=F.Ln, scale=math.exp(32.0))
+
+    def half(name, arrived, at):
+        op("v", "eq" + name, arrived + ["own"], v.tensor_tensor, out=T.eq[:, at:at + 64], in0=T.landy[:, at:at + 64],
+           in1=T.own[:, at:at + 64], op=A.is_equal)
+        op("v", "dec", ["ln" + name], v.tensor_scalar, out=T.dec[:, at // 8:at // 8 + 8], in0=T.lg[:, at // 8:at // 8 + 8],
+           scalar1=ROUND, scalar2=ROUND, op0=A.add, op1=A.subtract)
+        ps = T.pa2 if name == "n" else T.pa1
+        op("p", "cnt" + name, ["eq" + name, "m3"], p.matmul, out=ps[0:1, 0:64], lhsT=T.ones[:, 0:1], rhs=T.eq[:, at:at + 64],
+           start=True, stop=True)
+        op("v", "crun", ["cnt" + name, "keep"], v.tensor_tensor_scan, out=T.crun[0:1, at:at + 64], data0=T.keep[0:1, :],
+           data1=ps[0:1, 0:64], initial=0.0, op0=A.mult, op1=A.add)
+
+    share = 2 * rank
+    ln("lnn", ["yown"], T.lg[:, 2 * go:2 * go + 2], T.landy[:, og + share:og + share + 2])
+    for d, e in tod:
+        k = group[d]
+        ln("lnn", ["aydir"], T.lg[:, 2 * k:2 * k + 2], T.landy[:, 16 * k + share:16 * k + share + 2])
+    half("n", ["aydir", "yown"], na)
+    for j in range(2):
+        ln("lnf", ["ayrel"], T.lg[:, fa // 8 + j:fa // 8 + 8:2], T.landy[:, fa + share + j:fa + 64:16])
+    half("f", ["ayrel"], fa)
+    op("p", "psy", ["dec", "id32"], p.matmul, out=T.pa0[0:16, 0:128], lhsT=T.dec[:], rhs=T.id32[:], start=True, stop=True)
+    op("s", "yrow", ["psy"], s.activation, out=T.yrow[0:16, :], in_=T.pa0[0:16, 0:128], func=F.Copy, bias=float(V // 2))
     dma("s", "yout", ["yrow"], T.y[:], T.yrow[0:16, :])
-    op("v", "crun", ["cnt", "keep"], v.tensor_tensor_scan, out=T.crun[0:1, :], data0=T.keep[0:1, :], data1=T.ps1[0:1, 0:128],
-       initial=0.0, op0=A.mult, op1=A.add)
-    op("v", "crow", ["crun"], v.tensor_copy, out=T.crow[0:1, :], in_=T.crun[0:1, 15:128:16])
+    copy("v", "crow", ["crun"], T.crow[0:1, :], T.crun[0:1, 15:128:16])
     dma("y", "cout", ["crow"], T.cnt[:], T.crow[0:1, :])
-    R["finish"]()
-
-
-def send_two(R, T, g, topo, core, name, parts):
-    tr, total = [], 0
-    for jobs, rsem in parts:
-        for dst, out, src, eng in jobs:
-            rid, pid = topo.addr(dst, core)
-            tr.append(RemoteDMATransfer(dst_ids=[DstId(rid=rid, pnc=pid)], dma_engine_mask=sum(1 << e for e in eng),
-                                        remote_sem=T.sem[rsem], src=src, dst=out))
-            total += len(eng)
-    t = R["tag"](name)
-    t["n"] = total
-    g.remote_dma_fused(tr, local_sem=T.sem[t["sem"]])
+    finish()

@@ -4,13 +4,14 @@ from concourse.mybir import AluOpType as A, ActivationFunctionType as F
 
 V = 2048
 ROUND = 1.5 * 2.0 ** 18
-CUT1 = (576, 1280, 1792, V)
-CUT = (736, 1376, 1824, V)
-LAST = (("v", 0, 512), ("s", 1024, 1536), ("v", 512, 896), ("s", 1536, 1920), ("v", 896, 1024), ("s", 1920, 2048))
-ROWS = (("s", 0, 3, "pa0"), ("v", 3, 7, "pr0"), ("s", 7, 9, "pa1"), ("v", 9, 13, "pr1"), ("s", 13, 14, "pa2"), ("v", 14, 16, "pr2"))
-BACK = {"a": (0, 4, "pa0", "pr0"), "b": (4, 7, "pa1", "pr1"), "c": (7, 10, "pa2", "pr2"), "d": (10, 13, "pa0", "pr0"),
-        "e": (13, 16, "pa1", "pr1")}
-BACK_ORDER = {"v": "ga mb ma ge mc ca md me cd ce", "s": "gb gc gd cb cc", "p": "sb sa rb sc ra se sd rc rd re"}
+CUT1 = (928, 1536)
+CUT = (736, 1504)
+LAST = (("v", 0, 384), ("s", 1024, 1536), ("v", 384, 768), ("s", 1536, 1920), ("v", 768, 896), ("v", 896, 1024), ("s", 1920, 2048))
+ROWS = (("s", 0, 1, "pa0"), ("v", 1, 4, "pr0"), ("s", 4, 6, "pa1"), ("v", 6, 8, "pr1"))
+BACK = {"a": (0, 3, "pa0", "pr0"), "b": (3, 8, "pa1", "pr1"), "c": (8, 12, "pa2", "pr2"), "d": (12, 14, "pa0", "pr0"),
+        "e": (14, 16, "pa1", "pr1")}
+BACK_ORDER = {"v": "gb ma gd mb mc md cb me cc ce", "s": "ga gc ge ca cd", "p": "sa sb ra sc sd rb se rc rd re"}
+W = 24
 
 bf, f4, i4, u2 = "bfloat16", "float32", "int32", "uint16"
 SCRATCH = {
@@ -19,12 +20,15 @@ SCRATCH = {
     "w1p": ("sbuf", [128, 128], u2), "w1e": ("sbuf", [128, 128], u2), "w2p": ("sbuf", [128, 128], u2), "w2e": ("sbuf", [128, 128], u2),
     "stb": ("sbuf", [128, 128], bf),
     "ratio": ("sbuf", [128, 128], f4), "base": ("sbuf", [128, 128], bf), "ones": ("sbuf", [128, 128], bf),
-    "ident": ("sbuf", [128, 128], bf), "pick": ("sbuf", [128, 16], bf), "id32": ("sbuf", [128, 128], "float16"),
-    "reset": ("sbuf", [128, 256], bf), "keep": ("sbuf", [128, 64], bf), "own": ("sbuf", [128, 128], bf),
-    "pint": ("sbuf", [128, 16], i4), "pmod": ("sbuf", [128, 16], i4), "off1": ("sbuf", [128, 10], u2),
+    "ident": ("sbuf", [128, 128], bf), "pick": ("sbuf", [128, W], bf), "id32": ("sbuf", [128, 128], "float16"),
+    "reset": ("sbuf", [128, 8 * W], bf), "reset8": ("sbuf", [128, 128], bf), "keep": ("sbuf", [128, 64], bf),
+    "own": ("sbuf", [128, 128], bf), "other": ("sbuf", [128, 2], bf), "twice": ("sbuf", [128, 288], bf),
+    "pint": ("sbuf", [128, 18], i4), "pmod": ("sbuf", [128, 18], i4), "off1": ("sbuf", [128, 10], u2),
+    "peven": ("sbuf", [128, 18], i4), "zcol": ("sbuf", [128, 18], i4), "zsum": ("sbuf", [128, 18], i4),
+    "offz": ("sbuf", [128, 18], u2),
     "win1": ("sbuf", [128, V], bf), "win2": ("sbuf", [128, V], bf), "win3": ("sbuf", [128, V], bf),
-    "xu1": ("sbuf", [128, 2 * V], bf), "x2": ("sbuf", [128, V], bf), "x3": ("sbuf", [128, V], bf),
-    "s1": ("sbuf", [128, V], bf), "s2": ("sbuf", [128, V], bf), "s3": ("sbuf", [128, V], bf),
+    "xu1": ("sbuf", [128, 3 * V], bf), "x2": ("sbuf", [128, V], bf), "x3": ("sbuf", [128, V], bf),
+    "s2": ("sbuf", [128, V], bf), "s3": ("sbuf", [128, V], bf),
     "u2": ("sbuf", [128, V], bf), "u3": ("sbuf", [128, V], bf),
     "mine": ("sbuf", [128, 288], bf), "land": ("sbuf", [128, 288], bf),
     "ea": ("sbuf", [128, 32], bf), "eb": ("sbuf", [128, 16], bf), "erep": ("sbuf", [128, 144], bf),
@@ -187,9 +191,13 @@ def rank_program(g, core, T, topo):
        initial=math.exp(-129 / 32), op0=A.mult, op1=A.mult)
     op("g", "ident", ["ones"], g.affine_select, out=T.ident[:], in_=T.ones[:], pattern=[[-1, 128]], compare_op=A.is_equal,
        fill=0.0, base=0, channel_multiplier=1)
-    op("g", "pick", [], g.affine_select, out=T.pick[:], in_=T.ones[:, 0:16], pattern=[[0, 2], [-16, 8]],
+    pick8 = T.pick[:, 16:W]
+    op("g", "pick", [], g.affine_select, out=pick8, in_=T.ones[:, 0:8], pattern=[[-16, 8]],
        compare_op=A.is_equal, fill=0.0, base=0, channel_multiplier=1)
-    op("g", "pint", [], g.iota, out=T.pint[:], pattern=[[0, 16]], base=0, channel_multiplier=1)
+    op("g", "pick16", [], g.affine_select, out=T.pick[:, 0:16], in_=T.ones[:, 0:16], pattern=[[-16, 8], [-1, 2]],
+       compare_op=A.is_equal, fill=0.0, base=0, channel_multiplier=1)
+    op("g", "pint", [], g.iota, out=T.pint[:], pattern=[[0, 18]], base=0, channel_multiplier=1)
+    op("g", "zcol", [], g.iota, out=T.zcol[:], pattern=[[16, 2], [32, 9]], base=1, channel_multiplier=0)
     op("v", "zpad", [], v.memset, ap=T.mine[:], constant=0.0)
     op("v", "lpad", [], v.memset, ap=T.land[:, 256:288], constant=0.0)
     for i in range(16):
@@ -205,45 +213,42 @@ def rank_program(g, core, T, topo):
     send("cl2", [], [(cores[d], dd[go], l[group[d]], e[len(e) // 2 * k:len(e) // 2 * (k + 1)])
                      for k, (h, dd, l) in enumerate(two) for d, e in tod], "alist")
 
-    def starts(h, src, after):
-        for i in range(16):
-            op("p", ("fa%d" if i < 8 else "fb%d") % h, after, p.transpose, out=T.first[:, 128 * i:128 * i + 128],
-               in_=src[:, 2 * i + 1:2 * i + 257:2], identity=T.ident[:])
-
     def own_starts():
         copy("v", "stb", ["st"], T.stb[:], T.sti[:])
         op("p", "stt", ["stb", "ident"], p.transpose, out=T.pr0[:, 0:128], in_=T.stb[:], identity=T.ident[:])
         copy("v", "w1e", ["en"], T.w1e[:], T.eni[:])
         copy("v", "zs", ["stt", "zpad"], T.mine[:, 1:256:2], T.pr0[:, 0:128])
-        starts(1, T.mine, ["zs"])
+        k = CUT1[1] // 128
+        for i in range(16):
+            op("p", "fa1" if i < k else "fb1", ["zs"], p.transpose,
+               out=T.first[:, 128 * i:128 * i + 128] if i < k else T.pr2[:, 128 * (i - k):128 * (i - k + 1)],
+               in_=T.mine[:, 2 * i + 1:2 * i + 257:2], identity=T.ident[:])
 
-    def scatter_scan(h, win, wp, ready, x, sc, cut, first, between=None):
+    def scatter_scan(h, win, wp, ready, x, sc, at, cut, first, between=None):
         n = lambda t: t + str(h)
-        cuts = list(zip((0,) + cut[:-1], cut))
-        for k, (a, b) in enumerate(cuts):
-            if k:
-                copy("s", n("x%d" % k), ready + [wp[1]], x[:, a:b], win[:, 0:V].indirect(wp[0][:, a // 16:b // 16]))
-        if between:
-            between()
-        copy("v", n("x0"), ready + [wp[1]], x[:, 0:cut[0]], win[:, 0:V].indirect(wp[0][:, 0:cut[0] // 16]))
-        for k, (a, b) in enumerate(cuts):
-            op("v", n("sc%d" % k), [n("x%d" % k)] + first[:2 if k else 1] + ([n("sc%d" % (k - 1))] if k else []),
-               v.tensor_tensor_scan, out=sc[:, a:b], data0=T.first[:, a:b], data1=x[:, a:b],
-               initial=sc[:, a - 1:a] if k else 0.0, op0=A.add, op1=A.min)
-        return n("sc%d" % (len(cuts) - 1))
+        c1, c2 = cut
+        for q, a, b, t in (("s", 0, c1, "xa"), ("s", c2, V, "xb"), ("v", c1, c2, "xa")):
+            if q == "v" and between:
+                between()
+            copy(q, n(t), ready + [wp[1]], x[:, a:b], win[:, 0:V].indirect(wp[0][:, a // 16:b // 16]))
+        op("v", n("sa"), [n("xa"), first[0]], v.tensor_tensor_scan, out=sc[:, at:at + c2], data0=T.first[:, 0:c2],
+           data1=x[:, 0:c2], initial=0.0, op0=A.add, op1=A.min)
+        op("v", n("sb"), [n("xb"), n("sa"), first[1]], v.tensor_tensor_scan, out=sc[:, at + c2:at + V], data0=first[2],
+           data1=x[:, c2:V], initial=sc[:, at + c2 - 1:at + c2], op0=A.add, op1=A.min)
+        return n("sb")
 
-    def columns(h, sc, we, last, u, at, ps):
+    def columns(h, win, we, last, u, at, out):
         for q, a, b in LAST:
-            copy(q, "u%d_%d" % (h, a), [last, we[1]], u[:, at + a:at + b], sc[:, 0:V].indirect(we[0][:, a // 16:b // 16]))
+            copy(q, "u%d_%d" % (h, a), [last, we[1]], u[:, at + a:at + b], win.indirect(we[0][:, a // 16:b // 16]))
         for q, a, b in LAST:
             for i in range(a // 128, b // 128):
-                op("p", "sel%d" % h, ["u%d_%d" % (h, a), "pick"], p.matmul,
-                   out=ps[:, i:128:16] if h == 1 else ps[:, 8 * i:8 * i + 8],
-                   lhsT=u[:, at + 128 * i:at + 128 * i + 128], rhs=T.pick[:, 0:8], start=True, stop=True)
+                op("p", "sel%d" % h, ["u%d_%d" % (h, a), "pick"], p.matmul, out=out(i),
+                   lhsT=u[:, at + 128 * i:at + 128 * i + 128], rhs=pick8, start=True, stop=True)
 
     copy("v", "w1p", ["pm"], T.w1p[:], T.pmi[:])
-    last = scatter_scan(1, T.win1, (T.w1p, "w1p"), ["win1"], T.xu1, T.s1, CUT1, ["fa1", "fb1"], own_starts)
-    columns(1, T.s1, (T.w1e, "w1e"), last, T.xu1, V, T.pa0)
+    last = scatter_scan(1, T.win1, (T.w1p, "w1p"), ["win1"], T.xu1, T.xu1, 2 * V, CUT1,
+                        ["fa1", "fb1", T.pr2[:, 0:V - CUT1[1]]], own_starts)
+    columns(1, T.xu1[:, 2 * V:3 * V], (T.w1e, "w1e"), last, T.xu1, V, lambda i: T.pa0[:, 2 * (i % 8) + i // 8:128:16])
     fa = 16 * group[far[0]]
     na = 64 - fa
     og = 16 * go
@@ -258,15 +263,23 @@ def rank_program(g, core, T, topo):
     dma("y", "p2i", ["alist", "ownl"], T.p2i[:], T.dp[:])
     dma("y", "e2i", [], T.e2i[:], T.de[:])
     op("v", "pmod", ["pint"], v.tensor_scalar, out=T.pmod[:], in0=T.pint[:], scalar1=15, scalar2=None, op0=A.bitwise_and)
-    op("v", "reset0", [], v.memset, ap=T.reset[:], constant=0.0)
-    op("v", "keep0", [], v.memset, ap=T.keep[:], constant=1.0)
+    op("v", "peven", [], v.tensor_scalar, out=T.peven[:], in0=T.pint[:], scalar1=14, scalar2=None, op0=A.bitwise_and)
+    op("v", "zero", [], v.memset, ap=T.reset[:], constant=0.0)
+    op("v", "zero", [], v.memset, ap=T.reset8[:], constant=0.0)
+    op("v", "zero", [], v.memset, ap=T.keep[:], constant=1.0)
+    op("v", "zsum", ["peven", "zcol"], v.tensor_tensor, out=T.zsum[:], in0=T.peven[:], in1=T.zcol[:], op=A.add)
     op("v", "id32", [], v.tensor_scalar, out=T.id32[:], in0=T.ident[:], scalar1=32.0, scalar2=None, op0=A.mult)
     op("v", "off1", ["pmod"], v.tensor_scalar, out=T.off1[:], in0=T.pmod[:, 0:10], scalar1=1, scalar2=None, op0=A.mult)
-    op("v", "reset", ["reset0"], v.memset, ap=T.reset[:, 0:256:16], constant=1.0)
-    op("v", "keep", ["keep0"], v.memset, ap=T.keep[:, 0:64:16], constant=0.0)
+    for o in range(2):
+        op("v", "other", [], v.tensor_scalar, out=T.other[:, o:o + 1], in0=T.pmod[:, 0:1], scalar1=o, scalar2=None,
+           op0=A.not_equal)
+    copy("v", "offz", ["zsum"], T.offz[:], T.zsum[:])
+    op("v", "reset", ["zero"], v.memset, ap=T.reset[:, 0:8 * W:W], constant=1.0)
+    op("v", "reset", [], v.memset, ap=T.reset8[:, 0:128:8], constant=1.0)
+    op("v", "keep", [], v.memset, ap=T.keep[:, 0:64:16], constant=0.0)
     for i in range(16):
         op("p", "qown", [], p.matmul, out=T.pa1[:, i:128:16], lhsT=T.win1[:, 128 * i:128 * i + 128],
-           rhs=T.pick[:, 0:8], start=True, stop=True)
+           rhs=pick8, start=True, stop=True)
     copy("s", "own", ["qown"], T.own[:], T.pa1[:, 0:128])
 
     op("v", "ea", ["adir", "lown"], v.tensor_tensor, out=T.ea[:], in0=T.land[:, 2 * na:2 * na + 64:2],
@@ -280,17 +293,27 @@ def rank_program(g, core, T, topo):
        op=A.min)
     copy("v", "w2p", ["p2i"], T.w2p[:], T.p2i[:])
     copy("v", "w2e", ["e2i"], T.w2e[:], T.e2i[:])
+    copy("s", "twice", ["adir", "arel", "lown", "lpad", "offz"], T.twice[:], T.land[:, 0:288].indirect(T.offz[:, 0:18]))
     for q, a, b, ps in ROWS:
         for i in range(a, b):
-            o, l = T[ps][:, 128 * (i - a):128 * (i - a + 1)], T.b1[:, i:i + 128]
+            o, l = T[ps][:, 128 * (i - a):128 * (i - a + 1)], T.b1[:, 2 * i:2 * i + 128]
             if q == "v":
                 op("p", "row%d" % a, ["b1"], p.transpose, out=o, in_=l, identity=T.ident[:])
             else:
                 op("p", "row%d" % a, ["b1", "own"], p.matmul, out=o, lhsT=l, rhs=T.ident[:], start=True, stop=True)
-        copy(q, "win2", ["row%d" % a], T.win2[:, 128 * a:128 * b], T[ps][:, 0:128 * (b - a)])
-    starts(2, T.land, ["lpad"])
+        for o in range(2):
+            out, in_, col = T.win2[:, V // 2 * o + 128 * a:V // 2 * o + 128 * b], T[ps][:, 0:128 * (b - a)], T.other[:, o:o + 1]
+            if q == "v":
+                op(q, "win2", ["row%d" % a, "other"], v.tensor_scalar, out=out, in0=in_, scalar1=col, scalar2=None, op0=A.max)
+            else:
+                op(q, "win2", ["row%d" % a, "other"], s.activation, out=out, in_=in_, func=F.Identity, bias=col)
+    for i in range(16):
+        at = 144 * (i // 8) + 2 * (i % 8)
+        op("p", "f2", ["twice"], p.transpose, out=T.first[:, 128 * i:128 * i + 128], in_=T.twice[:, at:at + 128],
+           identity=T.ident[:])
+    first = ["f2", "f2", T.first[:, CUT[1]:V]]
 
-    last = scatter_scan(2, T.win2, (T.w2p, "w2p"), ["win2"], T.x2, T.s2, CUT, ["fa2", "fb2"])
+    last = scatter_scan(2, T.win2, (T.w2p, "w2p"), ["win2"], T.x2, T.s2, 0, CUT, first)
     names = list(BACK)
 
     def needs(c):
@@ -309,23 +332,23 @@ def rank_program(g, core, T, topo):
             copy(q, "bk" + c, [last, "w2e"], T.u2[:, 128 * a:128 * b], T.s2[:, 0:V].indirect(T.w2e[:, 8 * a:8 * b]))
         elif k == "s":
             for i in range(a, b):
-                op(q, "bk" + c, after, p.matmul, out=T[pa][:, 16 * (i - a):16 * (i - a + 1)],
+                op(q, "bk" + c, after + ["pick16"], p.matmul, out=T[pa][:, W * (i - a):W * (i - a + 1)],
                    lhsT=T.u2[:, 128 * i:128 * i + 128], rhs=T.pick[:], start=True, stop=True)
         elif k == "m":
-            op(q, "bk" + c, after + ["reset"], v.tensor_tensor_scan, out=T.xu1[:, 256 * a:256 * b:16],
-               data0=T.reset[:, 0:16 * (b - a)], data1=T[pa][:, 0:16 * (b - a)], initial=0.0, op0=A.add, op1=A.min)
+            op(q, "bk" + c, after + ["reset"], v.tensor_tensor_scan, out=T.xu1[:, 16 * W * a:16 * W * b:16],
+               data0=T.reset[:, 0:W * (b - a)], data1=T[pa][:, 0:W * (b - a)], initial=0.0, op0=A.add, op1=A.min)
         elif k == "r":
             for i in range(a, b):
                 op(q, "bk" + c, after, p.transpose, out=T[pr][:, 128 * (i - a):128 * (i - a + 1)],
-                   in_=T.xu1[:, 256 * i + 128:256 * i + 256], identity=T.ident[:])
+                   in_=T.xu1[:, 16 * W * (i + 1) - 128:16 * W * (i + 1)], identity=T.ident[:])
         else:
             copy(q, "bk" + c, after, T.win3[:, 128 * a:128 * b], T[pr][:, 0:128 * (b - a)])
 
     weave(BACK_ORDER, needs, emit)
 
-    last = scatter_scan(3, T.win3, (T.w2p, "w2p"), ["bkc" + x for x in names], T.x3, T.s3, CUT, ["fa2", "fb2"])
-    columns(3, T.s3, (T.w2e, "w2e"), last, T.u3, 0, T.pa1)
-    op("v", "m3", ["sel3"], v.tensor_tensor_scan, out=T.m3[:], data0=T.reset[:, 0:256:2], data1=T.pa1[:, 0:128], initial=0.0,
+    last = scatter_scan(3, T.win3, (T.w2p, "w2p"), ["bkc" + x for x in names], T.x3, T.s3, 0, CUT, first)
+    columns(3, T.s3[:, 0:V], (T.w2e, "w2e"), last, T.u3, 0, lambda i: T.pa1[:, 8 * i:8 * i + 8])
+    op("v", "m3", ["sel3"], v.tensor_tensor_scan, out=T.m3[:], data0=T.reset8[:], data1=T.pa1[:, 0:128], initial=0.0,
        op0=A.add, op1=A.min)
     copy("v", "yt", ["m3"], T.ytile[:], T.m3[:, 7:128:8])
     copy("v", "yown", ["m3"], T.landy[:, og:og + 16], T.m3[:, 7:128:8])

@@ -1,42 +1,40 @@
 import math
 from concourse.bass import DstId, RemoteDMATransfer
-from concourse.mybir import AluOpType as A, ActivationFunctionType as F
+from concourse.mybir import AluOpType as A, ActivationFunctionType as F, AxisListType
 
 V = 2048
-ROUND = 1.5 * 2.0 ** 18
-CUT1 = (928, 1536)
-CUT = (736, 1504)
-LAST = (("v", 0, 384), ("s", 1024, 1536), ("v", 384, 768), ("s", 1536, 1920), ("v", 768, 896), ("v", 896, 1024), ("s", 1920, 2048))
-ROWS = (("s", 0, 1, "pa0"), ("v", 1, 4, "pr0"), ("s", 4, 6, "pa1"), ("v", 6, 8, "pr1"))
-BACK = {"a": (0, 3, "pa0", "pr0"), "b": (3, 8, "pa1", "pr1"), "c": (8, 12, "pa2", "pr2"), "d": (12, 14, "pa0", "pr0"),
-        "e": (14, 16, "pa1", "pr1")}
-BACK_ORDER = {"v": "gb ma gd mb mc md cb me cc ce", "s": "ga gc ge ca cd", "p": "sa sb ra sc sd rb se rc rd re"}
+CUT1 = (544, 1152, 1344)
+CUT = (704, 1408, 1536)
+ROUND = 1.5 * 2.0 ** 23
+LAST = (("v", 0, 3), ("s", 3, 7), ("v", 7, 9), ("s", 9, 11), ("v", 11, 13), ("s", 13, 14), ("v", 14, 15), ("s", 15, 16))
+EARLY = 13
+ROWS = (("v", 0, 1, "pr0"), ("v", 1, 3, "pr1"), ("s", 3, 4, "pa0"), ("v", 4, 7, "pr2"), ("s", 7, 8, "pa1"))
+BACK = {"a": (0, 2), "b": (2, 5), "c": (5, 7), "d": (7, 8)}
+BACK_ORDER = {"v": "ha gb ma hc hd mb mc md cb cc", "s": "ga hb gc gd ca cd", "p": "sa sb ra sc sd rb rc rd"}
 W = 24
 
 bf, f4, i4, u2 = "bfloat16", "float32", "int32", "uint16"
 SCRATCH = {
-    "pmi": ("sbuf", [128, 128], i4), "eni": ("sbuf", [128, 128], i4), "sti": ("sbuf", [128, 128], i4),
+    "pmi": ("sbuf", [128, 128], i4), "sti": ("sbuf", [128, 128], i4),
     "p2i": ("sbuf", [128, 128], i4), "e2i": ("sbuf", [128, 128], i4),
     "w1p": ("sbuf", [128, 128], u2), "w1e": ("sbuf", [128, 128], u2), "w2p": ("sbuf", [128, 128], u2), "w2e": ("sbuf", [128, 128], u2),
     "stb": ("sbuf", [128, 128], bf),
     "ratio": ("sbuf", [128, 128], f4), "base": ("sbuf", [128, 128], bf), "ones": ("sbuf", [128, 128], bf),
     "ident": ("sbuf", [128, 128], bf), "pick": ("sbuf", [128, W], bf), "id32": ("sbuf", [128, 128], "float16"),
-    "reset": ("sbuf", [128, 8 * W], bf), "reset8": ("sbuf", [128, 128], bf), "keep": ("sbuf", [128, 64], bf),
-    "own": ("sbuf", [128, 128], bf), "other": ("sbuf", [128, 2], bf), "twice": ("sbuf", [128, 288], bf),
-    "pint": ("sbuf", [128, 18], i4), "pmod": ("sbuf", [128, 18], i4), "off1": ("sbuf", [128, 10], u2),
+    "reset": ("sbuf", [128, 4 * W], bf), "reset16": ("sbuf", [128, 256], bf),
+    "own": ("sbuf", [128, 16], bf), "other": ("sbuf", [128, 2], bf), "twice": ("sbuf", [128, 288], bf),
+    "pint": ("sbuf", [128, 18], i4), "pmod": ("sbuf", [128, 18], i4),
     "peven": ("sbuf", [128, 18], i4), "zcol": ("sbuf", [128, 18], i4), "zsum": ("sbuf", [128, 18], i4),
     "offz": ("sbuf", [128, 18], u2),
     "win1": ("sbuf", [128, V], bf), "win2": ("sbuf", [128, V], bf), "win3": ("sbuf", [128, V], bf),
     "xu1": ("sbuf", [128, 3 * V], bf), "x2": ("sbuf", [128, V], bf), "x3": ("sbuf", [128, V], bf),
     "s2": ("sbuf", [128, V], bf), "s3": ("sbuf", [128, V], bf),
     "u2": ("sbuf", [128, V], bf), "u3": ("sbuf", [128, V], bf),
-    "mine": ("sbuf", [128, 288], bf), "land": ("sbuf", [128, 288], bf),
-    "ea": ("sbuf", [128, 32], bf), "eb": ("sbuf", [128, 16], bf), "erep": ("sbuf", [128, 144], bf),
-    "ra": ("sbuf", [128, 32], bf), "rb": ("sbuf", [128, 16], bf), "b1": ("sbuf", [128, 144], bf),
-    "m3": ("sbuf", [128, 128], bf), "ytile": ("sbuf", [128, 16], bf), "landy": ("sbuf", [128, 128], bf),
-    "lg": ("sbuf", [128, 16], f4), "dec": ("sbuf", [128, 16], "float16"), "eq": ("sbuf", [128, 128], bf),
+    "mine": ("sbuf", [128, 128], bf), "land": ("sbuf", [128, 128], bf), "zs": ("sbuf", [128, 144], bf),
+    "stz": ("sbuf", [128, 288], bf), "hz": ("sbuf", [128, 32], bf),
+    "m3": ("sbuf", [128, 256], bf), "landy": ("sbuf", [128, 256], "float16"), "one16": ("sbuf", [128, 2], "float16"),
     "yrow": ("sbuf", [128, 128], f4), "crun": ("sbuf", [128, 128], f4), "crow": ("sbuf", [128, 8], f4),
-    "hu": ("sbuf", [128, 64], bf), "hy": ("sbuf", [128, 16], bf),
+    "hu": ("sbuf", [128, 32], bf), "hy": ("sbuf", [128, 32], "float16"),
     "lp": ("dram", [8, 128, 16], i4), "le": ("dram", [8, 128, 16], i4),
     "dp": ("dram", [8, 128, 16], i4), "de": ("dram", [8, 128, 16], i4),
     "hp": ("dram", [2, 128, 16], i4), "he": ("dram", [2, 128, 16], i4),
@@ -45,25 +43,24 @@ SCRATCH = {
     "pr0": ("psum", [128, 1024], bf), "pr1": ("psum", [128, 1024], bf), "pr2": ("psum", [128, 1024], bf),
 }
 NT = 138
-SEMAPHORES = ["t%d" % i for i in range(NT)] + ["alist", "adir", "arel", "aydir", "ayrel", "hlist", "hlab", "hfin"]
+SEMAPHORES = ["t%d" % i for i in range(NT)] + ["alist", "astart", "hstart", "amate", "adir", "arel", "aydir", "ayrel", "hlist", "hlab", "hfin"]
 
 
 def runner(g, T, topo, core):
     Q = {"g": g, "v": g.vector, "s": g.scalar, "p": g.tensor, "y": g.sync}
-    tags, know, count = {}, {k: set() for k in Q}, [0]
+    tags, know, count = {}, {k: set() for k in Q}, [0, 0]
 
     def tag(name, sem=None, n=0):
         if name not in tags:
             if sem is None:
                 sem = "t%d" % count[0]
                 count[0] += 1
-            tags[name] = {"sem": sem, "n": n, "know": set(), "waited": False}
+            tags[name] = {"sem": sem, "n": n, "know": set(), "waited": False, "age": 10 ** 6 + len(tags)}
         return tags[name]
 
     def wait(q, after):
-        for a in after:
-            if a in know[q]:
-                continue
+        need = [a for a in after if a not in know[q] and not any(a in tags[b]["know"] for b in after)]
+        for a in sorted(set(need), key=lambda a: tags[a]["age"]):
             t = tags[a]
             Q[q].wait_ge(T.sem[t["sem"]], t["n"])
             t["waited"] = True
@@ -72,6 +69,8 @@ def runner(g, T, topo, core):
     def raised(q, name, n):
         t = tag(name)
         assert not t["waited"], name
+        count[1] += 1
+        t["age"] = count[1]
         t["n"] += n
         t["know"] |= know[q]
         return T.sem[t["sem"]]
@@ -93,10 +92,10 @@ def runner(g, T, topo, core):
     def send(name, after, jobs, rsem):
         wait("g", after)
         tr, total = [], 0
-        for dst, out, src, eng in jobs:
+        for k, (dst, out, src, eng) in enumerate(jobs):
             rid, pid = topo.addr(dst, core)
             tr.append(RemoteDMATransfer(dst_ids=[DstId(rid=rid, pnc=pid)], dma_engine_mask=sum(1 << e for e in eng),
-                                        remote_sem=T.sem[rsem], src=src, dst=out))
+                                        remote_sem=T.sem[rsem if isinstance(rsem, str) else rsem[k]], src=src, dst=out))
             total += len(eng)
         g.remote_dma_fused(tr, local_sem=raised("g", name, total))
 
@@ -127,6 +126,7 @@ def helper_program(g, core, T, topo, q, mine):
     dst = [cores[d] for d in mine]
     e = topo.engines(core, dst[0])
     h, gq = len(e) // 2, group[q]
+    tag("hstart", "hstart", 8)
     tag("hlist", "hlist", 8)
     tag("hlab", "hlab", 8)
     tag("hfin", "hfin", 8)
@@ -135,9 +135,10 @@ def helper_program(g, core, T, topo, q, mine):
         k = e[h * i:h * i + h]
         jobs += [(dst[i], T.dp[gq], T.hp[i], k[0:2]), (dst[i], T.de[gq], T.he[i], k[2:4])]
     send("fl", ["hlist"], jobs, "alist")
-    send("fu", ["hlab"], [(dst[i], T.land[:, 32 * gq:32 * gq + 32], T.hu[:, 32 * i:32 * i + 32], e[h * i:h * i + h])
+    send("fs", ["hstart"], [(dst[i], T.stz[:, 32 * gq:32 * gq + 32], T.hz[:], e[h * i:h * i + h]) for i in range(2)], "astart")
+    send("fu", ["hlab"], [(dst[i], T.land[:, 16 * gq:16 * gq + 16], T.hu[:, 16 * i:16 * i + 16], e[h * i:h * i + h])
                           for i in range(2)], "arel")
-    send("fy", ["hfin"], [(dst[i], T.landy[:, 16 * gq:16 * gq + 16], T.hy[:], e[h * i:h * i + h]) for i in range(2)], "ayrel")
+    send("fy", ["hfin"], [(dst[i], T.landy[:, 32 * gq:32 * gq + 32], T.hy[:], e[h * i:h * i + h]) for i in range(2)], "ayrel")
     finish()
 
 
@@ -174,139 +175,142 @@ def rank_program(g, core, T, topo):
     allr = topo.engines(core, hs[0])
     on = [x for x in allr if x not in off]
     tod = [(mate, on), (plane[0], off[0:4]), (plane[1], off[4:8])]
-    for nm, n in (("alist", 32), ("adir", 16), ("arel", 16), ("aydir", 16), ("ayrel", 16)):
+    for nm, n in (("alist", 32), ("astart", 32), ("amate", 8), ("adir", 8), ("arel", 16), ("aydir", 16), ("ayrel", 16)):
         tag(nm, nm, n)
 
     dma("y", "pm", [], T.pmi[:], T.pm[:])
     dma("s", "st", [], T.sti[:], T.st[:])
     dma("y", "lists", [], T.lp[:], T.pm[:])
-    dma("s", "en", [], T.eni[:], T.en[:])
     dma("y", "lists", [], T.le[:], T.en[:])
     dma("y", "ownl", [], T.dp[go], T.pm[16 * go:16 * go + 16, :])
     dma("y", "ownl", [], T.de[go], T.en[16 * go:16 * go + 16, :])
 
-    op("v", "ones", [], v.memset, ap=T.ones[:], constant=1.0)
     op("v", "ratio", [], v.memset, ap=T.ratio[:], constant=math.exp(1 / 32))
-    op("v", "base", ["ones", "ratio"], v.tensor_tensor_scan, out=T.base[:], data0=T.ratio[:], data1=T.ones[:],
-       initial=math.exp(-129 / 32), op0=A.mult, op1=A.mult)
+    op("v", "ones", [], v.memset, ap=T.ones[:], constant=1.0)
+    op("v", "base", ["ratio"], v.tensor_tensor_scan, out=T.base[:], data0=T.ratio[:], data1=T.ratio[:],
+       initial=math.exp(-129 / 32), op0=A.mult, op1=A.min)
     op("g", "ident", ["ones"], g.affine_select, out=T.ident[:], in_=T.ones[:], pattern=[[-1, 128]], compare_op=A.is_equal,
        fill=0.0, base=0, channel_multiplier=1)
+    dma("g", "w1e", [], T.w1e[:], T.en[:])
     pick8 = T.pick[:, 16:W]
     op("g", "pick", [], g.affine_select, out=pick8, in_=T.ones[:, 0:8], pattern=[[-16, 8]],
        compare_op=A.is_equal, fill=0.0, base=0, channel_multiplier=1)
     op("g", "pick16", [], g.affine_select, out=T.pick[:, 0:16], in_=T.ones[:, 0:16], pattern=[[-16, 8], [-1, 2]],
        compare_op=A.is_equal, fill=0.0, base=0, channel_multiplier=1)
     op("g", "pint", [], g.iota, out=T.pint[:], pattern=[[0, 18]], base=0, channel_multiplier=1)
-    op("g", "zcol", [], g.iota, out=T.zcol[:], pattern=[[16, 2], [32, 9]], base=1, channel_multiplier=0)
-    op("v", "zpad", [], v.memset, ap=T.mine[:], constant=0.0)
-    op("v", "lpad", [], v.memset, ap=T.land[:, 256:288], constant=0.0)
+    op("g", "zcol", [], g.iota, out=T.zcol[:], pattern=[[8, 2], [32, 9]], base=16 * (go % 2), channel_multiplier=0)
+    op("v", "zpad", [], v.memset, ap=T.zs[:, 128:144], constant=0.0)
+    op("v", "lpad", [], v.memset, ap=T.stz[:, 256:288], constant=0.0)
     for i in range(16):
         o, c = T.win1[:, 128 * i:128 * i + 128], math.exp(4.0 * (i - 15))
-        if i % 8 < 5:
+        if i < 10:
             op("v", "win1", ["base"], v.tensor_scalar, out=o, in0=T.base[:], scalar1=c, scalar2=None, op0=A.mult)
         else:
             op("s", "win1", ["base"], s.activation, out=o, in_=T.base[:], func=F.Copy, scale=c)
 
-    two = ((T.hp, T.dp, T.lp), (T.he, T.de, T.le))
-    send("cl1", ["lists"], [(hs[i // 2], h[i % 2], l[group[d]], allr[8 * k + 2 * i:8 * k + 2 * i + 2])
-                            for k, (h, dd, l) in enumerate(two) for i, d in enumerate(far)], "hlist")
-    send("cl2", [], [(cores[d], dd[go], l[group[d]], e[len(e) // 2 * k:len(e) // 2 * (k + 1)])
-                     for k, (h, dd, l) in enumerate(two) for d, e in tod], "alist")
-
     def own_starts():
-        copy("v", "stb", ["st"], T.stb[:], T.sti[:])
         op("p", "stt", ["stb", "ident"], p.transpose, out=T.pr0[:, 0:128], in_=T.stb[:], identity=T.ident[:])
-        copy("v", "w1e", ["en"], T.w1e[:], T.eni[:])
-        copy("v", "zs", ["stt", "zpad"], T.mine[:, 1:256:2], T.pr0[:, 0:128])
+        copy("v", "zs", ["stt", "zpad"], T.zs[:, 0:128], T.pr0[:, 0:128])
         k = CUT1[1] // 128
         for i in range(16):
             op("p", "fa1" if i < k else "fb1", ["zs"], p.transpose,
                out=T.first[:, 128 * i:128 * i + 128] if i < k else T.pr2[:, 128 * (i - k):128 * (i - k + 1)],
-               in_=T.mine[:, 2 * i + 1:2 * i + 257:2], identity=T.ident[:])
+               in_=T.zs[:, i:i + 128], identity=T.ident[:])
+        two = ((T.hp, T.dp, T.lp), (T.he, T.de, T.le))
+        pair = lambda d: T.zs[:, 32 * (group[d] // 2):32 * (group[d] // 2) + 32]
+        send("cl1", ["lists"], [(hs[i // 2], h[i % 2], l[group[d]], allr[8 * k + 2 * i:8 * k + 2 * i + 2])
+                                for k, (h, dd, l) in enumerate(two) for i, d in enumerate(far)], "hlist")
+        send("cs1", ["zs"], [(hs[i], T.hz[:], pair(far[2 * i]), allr[8 * i:8 * i + 8]) for i in range(2)], "hstart")
+        send("cl2", [], [(cores[d], dd[go], l[group[d]], e[len(e) // 2 * k:len(e) // 2 * (k + 1)])
+                         for k, (h, dd, l) in enumerate(two) for d, e in tod], "alist")
+        send("cs2", [], [(cores[d], T.stz[:, 32 * go:32 * go + 32], pair(d), e) for d, e in tod], "astart")
 
     def scatter_scan(h, win, wp, ready, x, sc, at, cut, first, between=None):
         n = lambda t: t + str(h)
-        c1, c2 = cut
-        for q, a, b, t in (("s", 0, c1, "xa"), ("s", c2, V, "xb"), ("v", c1, c2, "xa")):
-            if q == "v" and between:
+        c1, c2, c3 = cut
+        for q, a, b, t in (("s", 0, c1, "xa"), ("s", c3, V, "xb"), ("v", c1, c2, "xa"), ("v", c2, c3, "xb")):
+            if q == "v" and between and a == c1:
                 between()
-            copy(q, n(t), ready + [wp[1]], x[:, a:b], win[:, 0:V].indirect(wp[0][:, a // 16:b // 16]))
+            if b > a:
+                copy(q, n(t), ready + [wp[1]], x[:, a:b], win[:, 0:V].indirect(wp[0][:, a // 16:b // 16]))
         op("v", n("sa"), [n("xa"), first[0]], v.tensor_tensor_scan, out=sc[:, at:at + c2], data0=T.first[:, 0:c2],
            data1=x[:, 0:c2], initial=0.0, op0=A.add, op1=A.min)
         op("v", n("sb"), [n("xb"), n("sa"), first[1]], v.tensor_tensor_scan, out=sc[:, at + c2:at + V], data0=first[2],
            data1=x[:, c2:V], initial=sc[:, at + c2 - 1:at + c2], op0=A.add, op1=A.min)
         return n("sb")
 
-    def columns(h, win, we, last, u, at, out):
+    def columns(h, win, we, last, u, at, pick, out):
         for q, a, b in LAST:
-            copy(q, "u%d_%d" % (h, a), [last, we[1]], u[:, at + a:at + b], win.indirect(we[0][:, a // 16:b // 16]))
+            copy(q, "u%d_%d" % (h, a), [last, we[1]], u[:, at + 128 * a:at + 128 * b], win.indirect(we[0][:, 8 * a:8 * b]))
         for q, a, b in LAST:
-            for i in range(a // 128, b // 128):
-                op("p", "sel%d" % h, ["u%d_%d" % (h, a), "pick"], p.matmul, out=out(i),
-                   lhsT=u[:, at + 128 * i:at + 128 * i + 128], rhs=pick8, start=True, stop=True)
+            for i in range(a, b):
+                op("p", "early" if h == 3 and i < EARLY else "sel%d" % h, ["u%d_%d" % (h, a), "pick"], p.matmul, out=out(i),
+                   lhsT=u[:, at + 128 * i:at + 128 * i + 128], rhs=pick, start=True, stop=True)
 
+    copy("v", "stb", ["st"], T.stb[:], T.sti[:])
     copy("v", "w1p", ["pm"], T.w1p[:], T.pmi[:])
     last = scatter_scan(1, T.win1, (T.w1p, "w1p"), ["win1"], T.xu1, T.xu1, 2 * V, CUT1,
                         ["fa1", "fb1", T.pr2[:, 0:V - CUT1[1]]], own_starts)
-    columns(1, T.xu1[:, 2 * V:3 * V], (T.w1e, "w1e"), last, T.xu1, V, lambda i: T.pa0[:, 2 * (i % 8) + i // 8:128:16])
+    columns(1, T.xu1[:, 2 * V:3 * V], (T.w1e, "w1e"), last, T.xu1, V, pick8, lambda i: T.pa0[:, i:128:16])
     fa = 16 * group[far[0]]
     na = 64 - fa
     og = 16 * go
-    copy("v", "minef", ["sel1"], T.mine[:, 2 * fa:2 * fa + 128:2], T.pa0[:, fa:fa + 64])
-    copy("v", "minen", ["sel1"], T.mine[:, 2 * na:2 * na + 128:2], T.pa0[:, na:na + 64])
-    send("sf", ["minef"], [(hs[i], T.hu[:], T.mine[:, 2 * fa + 64 * i:2 * fa + 64 * i + 64], allr[8 * i:8 * i + 8])
+    copy("v", "minef", ["sel1"], T.mine[:, fa:fa + 64], T.pa0[:, fa:fa + 64])
+    copy("v", "minen", ["sel1"], T.mine[:, na:na + 64], T.pa0[:, na:na + 64])
+    send("sf", ["minef"], [(hs[i], T.hu[:], T.mine[:, fa + 32 * i:fa + 32 * i + 32], allr[8 * i:8 * i + 8])
                            for i in range(2)], "hlab")
-    send("sn", ["minen"], [(cores[d], T.land[:, 2 * og:2 * og + 32], T.mine[:, 32 * group[d]:32 * group[d] + 32], e)
-                           for d, e in tod], "adir")
-    copy("v", "lown", ["minen"], T.land[:, 2 * og:2 * og + 32], T.mine[:, 2 * og:2 * og + 32])
+    send("sn", ["minen"], [(cores[d], T.land[:, og:og + 16], T.mine[:, 16 * group[d]:16 * group[d] + 16], e)
+                           for d, e in tod], ["amate", "adir", "adir"])
+    copy("v", "lown", [], T.stz[:, 2 * og:2 * og + 32], T.zs[:, 32 * (go // 2):32 * (go // 2) + 32])
 
     dma("y", "p2i", ["alist", "ownl"], T.p2i[:], T.dp[:])
     dma("y", "e2i", [], T.e2i[:], T.de[:])
     op("v", "pmod", ["pint"], v.tensor_scalar, out=T.pmod[:], in0=T.pint[:], scalar1=15, scalar2=None, op0=A.bitwise_and)
-    op("v", "peven", [], v.tensor_scalar, out=T.peven[:], in0=T.pint[:], scalar1=14, scalar2=None, op0=A.bitwise_and)
+    op("v", "peven", [], v.tensor_scalar, out=T.peven[:], in0=T.pint[:], scalar1=15, scalar2=1, op0=A.bitwise_and,
+       op1=A.logical_shift_right)
     op("v", "zero", [], v.memset, ap=T.reset[:], constant=0.0)
-    op("v", "zero", [], v.memset, ap=T.reset8[:], constant=0.0)
-    op("v", "zero", [], v.memset, ap=T.keep[:], constant=1.0)
+    op("v", "zero", [], v.memset, ap=T.reset16[:], constant=0.0)
     op("v", "zsum", ["peven", "zcol"], v.tensor_tensor, out=T.zsum[:], in0=T.peven[:], in1=T.zcol[:], op=A.add)
-    op("v", "id32", [], v.tensor_scalar, out=T.id32[:], in0=T.ident[:], scalar1=32.0, scalar2=None, op0=A.mult)
-    op("v", "off1", ["pmod"], v.tensor_scalar, out=T.off1[:], in0=T.pmod[:, 0:10], scalar1=1, scalar2=None, op0=A.mult)
+    copy("v", "one16", ["ones"], T.one16[:], T.ones[:, 0:2])
+    op("s", "id32", ["ident"], s.activation, out=T.id32[:], in_=T.ident[:], func=F.Ln, scale=math.exp(32.0), bias=1.0)
     for o in range(2):
-        op("v", "other", [], v.tensor_scalar, out=T.other[:, o:o + 1], in0=T.pmod[:, 0:1], scalar1=o, scalar2=None,
+        op("v", "other", ["pmod"], v.tensor_scalar, out=T.other[:, o:o + 1], in0=T.pmod[:, 0:1], scalar1=o, scalar2=None,
            op0=A.not_equal)
     copy("v", "offz", ["zsum"], T.offz[:], T.zsum[:])
-    op("v", "reset", ["zero"], v.memset, ap=T.reset[:, 0:8 * W:W], constant=1.0)
-    op("v", "reset", [], v.memset, ap=T.reset8[:, 0:128:8], constant=1.0)
-    op("v", "keep", [], v.memset, ap=T.keep[:, 0:64:16], constant=0.0)
+    op("v", "reset", ["zero"], v.memset, ap=T.reset[:, 0:4 * W:W], constant=1.0)
+    op("v", "reset", [], v.memset, ap=T.reset16[:, 0:256:16], constant=1.0)
     for i in range(16):
-        op("p", "qown", [], p.matmul, out=T.pa1[:, i:128:16], lhsT=T.win1[:, 128 * i:128 * i + 128],
-           rhs=pick8, start=True, stop=True)
-    copy("s", "own", ["qown"], T.own[:], T.pa1[:, 0:128])
+        op("p", "qown", [], p.matmul, out=T.pa1[:, i:i + 1], lhsT=T.win1[:, 128 * i:128 * i + 128],
+           rhs=T.pick[:, 16:17], start=True, stop=True)
+    copy("s", "own", ["qown"], T.own[:], T.pa1[:, 0:16])
 
-    op("v", "ea", ["adir", "lown"], v.tensor_tensor, out=T.ea[:], in0=T.land[:, 2 * na:2 * na + 64:2],
-       in1=T.land[:, 2 * na + 64:2 * na + 128:2], op=A.min)
-    op("v", "eb", ["ea"], v.tensor_tensor, out=T.eb[:], in0=T.ea[:, 0:16], in1=T.ea[:, 16:32], op=A.min)
-    copy("v", "erep", ["eb", "off1"], T.erep[:], T.eb[:, 0:16].indirect(T.off1[:, 0:9]))
-    op("v", "ra", ["arel"], v.tensor_tensor, out=T.ra[:], in0=T.land[:, 2 * fa:2 * fa + 64:2],
-       in1=T.land[:, 2 * fa + 64:2 * fa + 128:2], op=A.min)
-    op("v", "rb", ["ra"], v.tensor_tensor, out=T.rb[:], in0=T.ra[:, 0:16], in1=T.ra[:, 16:32], op=A.min)
-    op("v", "b1", ["rb", "erep"], v.tensor_tensor, out=T.b1[:], in0=T.rb[:, 0:16].indirect(T.off1[:, 0:9]), in1=T.erep[:],
-       op=A.min)
+    def halves(q, name, after, win, a, b, ps):
+        for o in range(2):
+            out, in_, col = win[:, V // 2 * o + 128 * a:V // 2 * o + 128 * b], ps[:, 0:128 * (b - a)], T.other[:, o:o + 1]
+            if q == "v":
+                op(q, name, after + ["other"], v.tensor_scalar, out=out, in0=in_, scalar1=col, scalar2=None, op0=A.max)
+            else:
+                op(q, name, after + ["other"], s.activation, out=out, in_=in_, func=F.Identity, bias=col)
+
+    copy("s", "twice", ["astart", "lown", "lpad", "offz"], T.twice[:], T.stz[:, 0:288].indirect(T.offz[:, 0:18]))
+    labels = lambda d: T.land[:, 16 * group[d]:16 * group[d] + 16]
+    side = [(t, T.mine[:, og:og + 16], "minen") for t in [0] + list(range(8, 16))] + [(1, labels(mate), "amate")]
+    side += [(2 + k, labels(d), "adir") for k, d in enumerate(plane)] + [(4 + k, labels(d), "arel") for k, d in enumerate(far)]
+    for t, src, after in side:
+        op("p", "side", [after], p.matmul, out=T.pa2[:, t:256:16], lhsT=T.ident[:], rhs=src, start=True, stop=True)
+    for o in range(2):
+        op("v", "b1", ["side", "reset"], v.tensor_tensor_scan, out=T.xu1[:, o:V:16], data0=T.reset16[:, 0:128],
+           data1=T.pa2[:, 128 * o:128 * o + 128], initial=0.0, op0=A.add, op1=A.min)
     copy("v", "w2p", ["p2i"], T.w2p[:], T.p2i[:])
     copy("v", "w2e", ["e2i"], T.w2e[:], T.e2i[:])
-    copy("s", "twice", ["adir", "arel", "lown", "lpad", "offz"], T.twice[:], T.land[:, 0:288].indirect(T.offz[:, 0:18]))
     for q, a, b, ps in ROWS:
         for i in range(a, b):
-            o, l = T[ps][:, 128 * (i - a):128 * (i - a + 1)], T.b1[:, 2 * i:2 * i + 128]
+            o, l = T[ps][:, 128 * (i - a):128 * (i - a + 1)], T.xu1[:, 256 * i + 128:256 * i + 256]
             if q == "v":
                 op("p", "row%d" % a, ["b1"], p.transpose, out=o, in_=l, identity=T.ident[:])
             else:
                 op("p", "row%d" % a, ["b1", "own"], p.matmul, out=o, lhsT=l, rhs=T.ident[:], start=True, stop=True)
-        for o in range(2):
-            out, in_, col = T.win2[:, V // 2 * o + 128 * a:V // 2 * o + 128 * b], T[ps][:, 0:128 * (b - a)], T.other[:, o:o + 1]
-            if q == "v":
-                op(q, "win2", ["row%d" % a, "other"], v.tensor_scalar, out=out, in0=in_, scalar1=col, scalar2=None, op0=A.max)
-            else:
-                op(q, "win2", ["row%d" % a, "other"], s.activation, out=out, in_=in_, func=F.Identity, bias=col)
+        halves(q, "win2", ["row%d" % a], T.win2, a, b, T[ps])
     for i in range(16):
         at = 144 * (i // 8) + 2 * (i % 8)
         op("p", "f2", ["twice"], p.transpose, out=T.first[:, 128 * i:128 * i + 128], in_=T.twice[:, at:at + 128],
@@ -318,70 +322,70 @@ def rank_program(g, core, T, topo):
 
     def needs(c):
         k, x = c[0], c[1]
-        if k == "g":
-            return []
-        bank = {"s": 2, "r": 3}.get(k)
-        prev = [y for y in names[:names.index(x)] if bank and BACK[y][bank] == BACK[x][bank]]
-        return [{"s": "g", "m": "s", "r": "m", "c": "r"}[k] + x] + [{"s": "m", "r": "c"}[k] + y for y in prev]
+        out = [t + x for t in {"g": "", "h": "", "s": "gh", "m": "s", "r": "m", "c": "r"}[k]]
+        if k in "sr" and names.index(x) >= 3:
+            out.append({"s": "m", "r": "c"}[k] + names[names.index(x) - 3])
+        return out
 
     def emit(q, c):
         k, x = c[0], c[1]
-        a, b, pa, pr = BACK[x]
-        after = ["bk" + n for n in needs(c)]
-        if k == "g":
+        a, b = BACK[x]
+        n, pa, pr = b - a, T["pa%d" % (names.index(x) % 3)], T["pr%d" % (names.index(x) % 3)]
+        after = ["bk" + t for t in needs(c)]
+        if k in "gh":
+            a, b = (a, b) if k == "g" else (a + 8, b + 8)
             copy(q, "bk" + c, [last, "w2e"], T.u2[:, 128 * a:128 * b], T.s2[:, 0:V].indirect(T.w2e[:, 8 * a:8 * b]))
         elif k == "s":
-            for i in range(a, b):
-                op(q, "bk" + c, after + ["pick16"], p.matmul, out=T[pa][:, W * (i - a):W * (i - a + 1)],
+            for j, i in enumerate(list(range(a, b)) + list(range(a + 8, b + 8))):
+                op(q, "bk" + c, after + ["pick16"], p.matmul, out=pa[:, W * j:W * j + W],
                    lhsT=T.u2[:, 128 * i:128 * i + 128], rhs=T.pick[:], start=True, stop=True)
         elif k == "m":
-            op(q, "bk" + c, after + ["reset"], v.tensor_tensor_scan, out=T.xu1[:, 16 * W * a:16 * W * b:16],
-               data0=T.reset[:, 0:W * (b - a)], data1=T[pa][:, 0:W * (b - a)], initial=0.0, op0=A.add, op1=A.min)
+            for o in range(2):
+                op(q, "bk" + c, after + ["reset"], v.tensor_tensor_scan, out=T.xu1[:, 16 * W * a + o:16 * W * b:16],
+                   data0=T.reset[:, 0:W * n], data1=pa[:, W * n * o:W * n * (o + 1)], initial=0.0, op0=A.add, op1=A.min)
         elif k == "r":
             for i in range(a, b):
-                op(q, "bk" + c, after, p.transpose, out=T[pr][:, 128 * (i - a):128 * (i - a + 1)],
+                op(q, "bk" + c, after, p.transpose, out=pr[:, 128 * (i - a):128 * (i - a + 1)],
                    in_=T.xu1[:, 16 * W * (i + 1) - 128:16 * W * (i + 1)], identity=T.ident[:])
         else:
-            copy(q, "bk" + c, after, T.win3[:, 128 * a:128 * b], T[pr][:, 0:128 * (b - a)])
+            halves(q, "bk" + c if c == "ca" else "win3", after, T.win3, a, b, pr)
 
     weave(BACK_ORDER, needs, emit)
 
-    last = scatter_scan(3, T.win3, (T.w2p, "w2p"), ["bkc" + x for x in names], T.x3, T.s3, 0, CUT, first)
-    columns(3, T.s3[:, 0:V], (T.w2e, "w2e"), last, T.u3, 0, lambda i: T.pa1[:, 8 * i:8 * i + 8])
-    op("v", "m3", ["sel3"], v.tensor_tensor_scan, out=T.m3[:], data0=T.reset8[:], data1=T.pa1[:, 0:128], initial=0.0,
-       op0=A.add, op1=A.min)
-    copy("v", "yt", ["m3"], T.ytile[:], T.m3[:, 7:128:8])
-    copy("v", "yown", ["m3"], T.landy[:, og:og + 16], T.m3[:, 7:128:8])
-
-    send("yf", ["yt"], [(hs[i], T.hy[:], T.ytile[:], allr[8 * i:8 * i + 8]) for i in range(2)], "hfin")
-    send("yn", ["yt"], [(cores[d], T.landy[:, og:og + 16], T.ytile[:], e) for d, e in tod], "aydir")
-
-    def ln(name, after, out, in_):
-        op("s", name, after, s.activation, out=out, in_=in_, func=F.Ln, scale=math.exp(32.0))
-
-    def half(name, arrived, at):
-        op("v", "eq" + name, arrived + ["own"], v.tensor_tensor, out=T.eq[:, at:at + 64], in0=T.landy[:, at:at + 64],
-           in1=T.own[:, at:at + 64], op=A.is_equal)
-        op("v", "dec", ["ln" + name], v.tensor_scalar, out=T.dec[:, at // 8:at // 8 + 8], in0=T.lg[:, at // 8:at // 8 + 8],
-           scalar1=ROUND, scalar2=ROUND, op0=A.add, op1=A.subtract)
-        ps = T.pa2 if name == "n" else T.pa1
-        op("p", "cnt" + name, ["eq" + name, "m3"], p.matmul, out=ps[0:1, 0:64], lhsT=T.ones[:, 0:1], rhs=T.eq[:, at:at + 64],
-           start=True, stop=True)
-        op("v", "crun", ["cnt" + name, "keep"], v.tensor_tensor_scan, out=T.crun[0:1, at:at + 64], data0=T.keep[0:1, :],
-           data1=ps[0:1, 0:64], initial=0.0, op0=A.mult, op1=A.add)
-
-    share = 2 * rank
-    ln("lnn", ["yown"], T.lg[:, 2 * go:2 * go + 2], T.landy[:, og + share:og + share + 2])
-    for d, e in tod:
-        k = group[d]
-        ln("lnn", ["aydir"], T.lg[:, 2 * k:2 * k + 2], T.landy[:, 16 * k + share:16 * k + share + 2])
-    half("n", ["aydir", "yown"], na)
+    last = scatter_scan(3, T.win3, (T.w2p, "w2p"), ["bkca", "win3"], T.x3, T.s3, 0, CUT, first)
+    columns(3, T.s3[:, 0:V], (T.w2e, "w2e"), last, T.u3, 0, T.pick[:, 0:16],
+            lambda i: (T.pa1 if i < EARLY else T.pa2)[:, 16 * i:16 * i + 16])
+    for after, ps, a, b in (("early", T.pa1, 0, 16 * EARLY), ("sel3", T.pa2, 16 * EARLY, 256)):
+        op("v", "m3", [after], v.tensor_tensor_scan, out=T.m3[:, a:b], data0=T.reset16[:, a:b], data1=ps[:, a:b], initial=0.0,
+           op0=A.add, op1=A.min)
+    tile = T.landy[:, 2 * og:2 * og + 32]
     for j in range(2):
-        ln("lnf", ["ayrel"], T.lg[:, fa // 8 + j:fa // 8 + 8:2], T.landy[:, fa + share + j:fa + 64:16])
-    half("f", ["ayrel"], fa)
-    op("p", "psy", ["dec", "id32"], p.matmul, out=T.pa0[0:16, 0:128], lhsT=T.dec[:], rhs=T.id32[:], start=True, stop=True)
-    op("s", "yrow", ["psy"], s.activation, out=T.yrow[0:16, :], in_=T.pa0[0:16, 0:128], func=F.Copy, bias=float(V // 2))
-    dma("s", "yout", ["yrow"], T.y[:], T.yrow[0:16, :])
-    copy("v", "crow", ["crun"], T.crow[0:1, :], T.crun[0:1, 15:128:16])
-    dma("y", "cout", ["crow"], T.cnt[:], T.crow[0:1, :])
+        op("s", "yt", ["m3"], s.activation, out=T.landy[:, 2 * og + 16 * j:2 * og + 16 * j + 16:2],
+           in_=T.m3[:, 15 + 16 * j:256:32], func=F.Ln, scale=math.exp(32.0))
+    op("v", "yt", ["m3", "own"], v.tensor_tensor, out=T.landy[:, 2 * og + 1:2 * og + 32:2], in0=T.m3[:, 15:256:16],
+       in1=T.own[:], op=A.is_equal)
+
+    send("yf", ["yt"], [(hs[i], T.hy[:], tile, allr[8 * i:8 * i + 8]) for i in range(2)], "hfin")
+    send("yn", [], [(cores[d], tile, tile, e) for d, e in tod], "aydir")
+
+    def count(name, arrived, k0):
+        for q, a, b, ps in (("s", k0, k0 + 3, T.pa2), ("v", k0 + 3, k0 + 4, T.pa1)):
+            op("p", "cnt" + q + name, arrived, p.matmul, out=ps[0:1, 0:16 * (b - a)], lhsT=T.one16[:, 0:1],
+               rhs=T.landy[:, 32 * a + 1:32 * b:2], start=True, stop=True)
+            for k in range(a, b):
+                in_, out = ps[0:1, 16 * (k - a):16 * (k - a + 1)], T.crow[0:1, k:k + 1]
+                if q == "v":
+                    op(q, "crow" + name, ["cnt" + q + name], v.tensor_reduce, out=out, in_=in_, axis=AxisListType.X, op=A.add)
+                else:
+                    op(q, "crow" + name, ["cnt" + q + name], s.activation, out=T.crun[0:1, 16 * k:16 * k + 16], in_=in_,
+                       func=F.Copy, accum_out=out)
+
+    count("n", ["aydir", "yt", "one16", "id32"], na // 16)
+    count("f", ["crown", "ayrel"], fa // 16)
+    op("p", "psy", ["id32"], p.matmul, out=T.pa0[0:16, 0:128], lhsT=T.landy[:, 2 * rank:256:16], rhs=T.id32[:],
+       start=True, stop=True)
+    op("v", "yrow", ["psy"], v.tensor_scalar, out=T.yrow[0:16, :], in0=T.pa0[0:16, 0:128], scalar1=ROUND,
+       scalar2=ROUND - V // 2, op0=A.add, op1=A.subtract)
+    dma("y", "yout", ["yrow"], T.y[:], T.yrow[0:16, :])
+    dma("s", "cout", ["crown", "crowf"], T.cnt[:], T.crow[0:1, :])
     finish()

import math
from concourse.bass import DstId, RemoteDMATransfer
from concourse.mybir import AluOpType as A, ActivationFunctionType as F, AxisListType

V = 2048
CUT1 = (544, 1152, 1344)
CUT = (704, 1408, 1536)
ROUND = 1.5 * 2.0 ** 23
LAST = (("v", 0, 3), ("s", 3, 7), ("v", 7, 9), ("s", 9, 11), ("v", 11, 13), ("s", 13, 14), ("v", 14, 15), ("s", 15, 16))
EARLY = 13
ROWS = (("v", 0, 1, "pr0"), ("v", 1, 3, "pr1"), ("s", 3, 4, "pa0"), ("v", 4, 7, "pr2"), ("s", 7, 8, "pa1"))
BACK = {"a": (0, 2), "b": (2, 5), "c": (5, 7), "d": (7, 8)}
BACK_ORDER = {"v": "ha gb ma hc hd mb mc md cb cc", "s": "ga hb gc gd ca cd", "p": "sa sb ra sc sd rb rc rd"}
W = 24

bf, f4, i4, u2 = "bfloat16", "float32", "int32", "uint16"
SCRATCH = {
    "pmi": ("sbuf", [128, 128], i4), "sti": ("sbuf", [128, 128], i4),
    "p2i": ("sbuf", [128, 128], i4), "e2i": ("sbuf", [128, 128], i4),
    "w1p": ("sbuf", [128, 128], u2), "w1e": ("sbuf", [128, 128], u2), "w2p": ("sbuf", [128, 128], u2), "w2e": ("sbuf", [128, 128], u2),
    "stb": ("sbuf", [128, 128], bf),
    "ratio": ("sbuf", [128, 128], f4), "base": ("sbuf", [128, 128], bf), "ones": ("sbuf", [128, 128], bf),
    "ident": ("sbuf", [128, 128], bf), "pick": ("sbuf", [128, W], bf), "id32": ("sbuf", [128, 128], "float16"),
    "reset": ("sbuf", [128, 4 * W], bf), "reset16": ("sbuf", [128, 256], bf),
    "own": ("sbuf", [128, 16], bf), "other": ("sbuf", [128, 2], bf), "twice": ("sbuf", [128, 288], bf),
    "pint": ("sbuf", [128, 18], i4), "pmod": ("sbuf", [128, 18], i4),
    "peven": ("sbuf", [128, 18], i4), "zcol": ("sbuf", [128, 18], i4), "zsum": ("sbuf", [128, 18], i4),
    "offz": ("sbuf", [128, 18], u2),
    "win1": ("sbuf", [128, V], bf), "win2": ("sbuf", [128, V], bf), "win3": ("sbuf", [128, V], bf),
    "xu1": ("sbuf", [128, 3 * V], bf), "x2": ("sbuf", [128, V], bf), "x3": ("sbuf", [128, V], bf),
    "s2": ("sbuf", [128, V], bf), "s3": ("sbuf", [128, V], bf),
    "u2": ("sbuf", [128, V], bf), "u3": ("sbuf", [128, V], bf),
    "mine": ("sbuf", [128, 128], bf), "land": ("sbuf", [128, 128], bf), "zs": ("sbuf", [128, 144], bf),
    "stz": ("sbuf", [128, 288], bf), "hz": ("sbuf", [128, 32], bf),
    "m3": ("sbuf", [128, 256], bf), "landy": ("sbuf", [128, 256], "float16"), "one16": ("sbuf", [128, 2], "float16"),
    "yrow": ("sbuf", [128, 128], f4), "crun": ("sbuf", [128, 128], f4), "crow": ("sbuf", [128, 8], f4),
    "hu": ("sbuf", [128, 32], bf), "hy": ("sbuf", [128, 32], "float16"),
    "lp": ("dram", [8, 128, 16], i4), "le": ("dram", [8, 128, 16], i4),
    "dp": ("dram", [8, 128, 16], i4), "de": ("dram", [8, 128, 16], i4),
    "hp": ("dram", [2, 128, 16], i4), "he": ("dram", [2, 128, 16], i4),
    "first": ("psum", [128, V], bf),
    "pa0": ("psum", [128, 512], f4), "pa1": ("psum", [128, 512], f4), "pa2": ("psum", [128, 512], f4),
    "pr0": ("psum", [128, 1024], bf), "pr1": ("psum", [128, 1024], bf), "pr2": ("psum", [128, 1024], bf),
}
NT = 138
SEMAPHORES = ["t%d" % i for i in range(NT)] + ["alist", "astart", "hstart", "amate", "adir", "arel", "aydir", "ayrel", "hlist", "hlab", "hfin"]


def runner(g, T, topo, core):
    Q = {"g": g, "v": g.vector, "s": g.scalar, "p": g.tensor, "y": g.sync}
    tags, know, count = {}, {k: set() for k in Q}, [0, 0]

    def tag(name, sem=None, n=0):
        if name not in tags:
            if sem is None:
                sem = "t%d" % count[0]
                count[0] += 1
            tags[name] = {"sem": sem, "n": n, "know": set(), "waited": False, "age": 10 ** 6 + len(tags)}
        return tags[name]

    def wait(q, after):
        need = [a for a in after if a not in know[q] and not any(a in tags[b]["know"] for b in after)]
        for a in sorted(set(need), key=lambda a: tags[a]["age"]):
            t = tags[a]
            Q[q].wait_ge(T.sem[t["sem"]], t["n"])
            t["waited"] = True
            know[q] |= {a} | t["know"]

    def raised(q, name, n):
        t = tag(name)
        assert not t["waited"], name
        count[1] += 1
        t["age"] = count[1]
        t["n"] += n
        t["know"] |= know[q]
        return T.sem[t["sem"]]

    def op(q, name, after, call, **kw):
        wait(q, after)
        call(**kw).then_inc(raised(q, name, 1), 1)

    def copy(q, name, after, out, in_):
        if q == "v":
            op(q, name, after, g.vector.tensor_copy, out=out, in_=in_)
        else:
            op(q, name, after, g.scalar.activation, out=out, in_=in_, func=F.Copy)

    def dma(q, name, after, out, in_):
        wait(q, after)
        Q[q].dma_start(out=out, in_=in_).then_inc(raised(q, name, 16), 16)

    def send(name, after, jobs, rsem):
        wait("g", after)
        tr, total = [], 0
        for k, (dst, out, src, eng) in enumerate(jobs):
            rid, pid = topo.addr(dst, core)
            tr.append(RemoteDMATransfer(dst_ids=[DstId(rid=rid, pnc=pid)], dma_engine_mask=sum(1 << e for e in eng),
                                        remote_sem=T.sem[rsem if isinstance(rsem, str) else rsem[k]], src=src, dst=out))
            total += len(eng)
        g.remote_dma_fused(tr, local_sem=raised("g", name, total))

    def finish():
        wait("g", [a for a in tags if not tags[a]["waited"]])

    return tag, op, copy, dma, send, finish


def plan(T, topo):
    cores = T.cores
    near = [[p for p in range(len(cores)) if cores[p] in topo.cores_of(cores[q]) or topo.same_plane(cores[q], cores[p])]
            for q in range(len(cores))]
    owners = near[0] + [p for p in range(len(cores)) if p not in near[0]]
    group = {p: k for k, p in enumerate(owners)}
    return cores, near, owners, group


def helpers(T, topo, q, far):
    c = T.cores[q]
    return [h for h in topo.cores_of(c) if T.rank_of(h) is None and topo.die(h) == topo.die(c)
            and all(topo.may_write(h, T.cores[d]) for d in far)][:2]


def helper_program(g, core, T, topo, q, mine):
    tag, op, copy, dma, send, finish = runner(g, T, topo, core)
    cores, near, owners, group = plan(T, topo)
    dst = [cores[d] for d in mine]
    e = topo.engines(core, dst[0])
    h, gq = len(e) // 2, group[q]
    tag("hstart", "hstart", 8)
    tag("hlist", "hlist", 8)
    tag("hlab", "hlab", 8)
    tag("hfin", "hfin", 8)
    jobs = []
    for i in range(2):
        k = e[h * i:h * i + h]
        jobs += [(dst[i], T.dp[gq], T.hp[i], k[0:2]), (dst[i], T.de[gq], T.he[i], k[2:4])]
    send("fl", ["hlist"], jobs, "alist")
    send("fs", ["hstart"], [(dst[i], T.stz[:, 32 * gq:32 * gq + 32], T.hz[:], e[h * i:h * i + h]) for i in range(2)], "astart")
    send("fu", ["hlab"], [(dst[i], T.land[:, 16 * gq:16 * gq + 16], T.hu[:, 16 * i:16 * i + 16], e[h * i:h * i + h])
                          for i in range(2)], "arel")
    send("fy", ["hfin"], [(dst[i], T.landy[:, 32 * gq:32 * gq + 32], T.hy[:], e[h * i:h * i + h]) for i in range(2)], "ayrel")
    finish()


def weave(orders, needs, emit):
    left = {q: o.split() for q, o in orders.items()}
    done = set()
    while any(left.values()):
        q = [q for q in left if left[q] and all(n in done for n in needs(left[q][0]))][0]
        name = left[q].pop(0)
        emit(q, name)
        done.add(name)


def rank_program(g, core, T, topo):
    cores, near, owners, group = plan(T, topo)
    rank = T.rank_of(core)
    if rank is None:
        for q in range(len(cores)):
            if core in topo.cores_of(cores[q]):
                far = [d for d in owners if d not in near[q]]
                hs = helpers(T, topo, q, far)
                if core in hs:
                    i = hs.index(core)
                    helper_program(g, core, T, topo, q, far[2 * i:2 * i + 2])
        return
    tag, op, copy, dma, send, finish = runner(g, T, topo, core)
    v, s, p = g.vector, g.scalar, g.tensor
    go = group[rank]
    far = [d for d in owners if d not in near[rank]]
    hs = helpers(T, topo, rank, far)
    mate = [d for d in near[rank] if d != rank and cores[d] in topo.cores_of(core)][0]
    plane = [d for d in near[rank] if d != rank and d != mate]
    off = topo.engines(core, cores[plane[0]])
    allr = topo.engines(core, hs[0])
    on = [x for x in allr if x not in off]
    tod = [(mate, on), (plane[0], off[0:4]), (plane[1], off[4:8])]
    for nm, n in (("alist", 32), ("astart", 32), ("amate", 8), ("adir", 8), ("arel", 16), ("aydir", 16), ("ayrel", 16)):
        tag(nm, nm, n)

    dma("y", "pm", [], T.pmi[:], T.pm[:])
    dma("s", "st", [], T.sti[:], T.st[:])
    dma("y", "lists", [], T.lp[:], T.pm[:])
    dma("y", "lists", [], T.le[:], T.en[:])
    dma("y", "ownl", [], T.dp[go], T.pm[16 * go:16 * go + 16, :])
    dma("y", "ownl", [], T.de[go], T.en[16 * go:16 * go + 16, :])

    op("v", "ratio", [], v.memset, ap=T.ratio[:], constant=math.exp(1 / 32))
    op("v", "ones", [], v.memset, ap=T.ones[:], constant=1.0)
    op("v", "base", ["ratio"], v.tensor_tensor_scan, out=T.base[:], data0=T.ratio[:], data1=T.ratio[:],
       initial=math.exp(-129 / 32), op0=A.mult, op1=A.min)
    op("g", "ident", ["ones"], g.affine_select, out=T.ident[:], in_=T.ones[:], pattern=[[-1, 128]], compare_op=A.is_equal,
       fill=0.0, base=0, channel_multiplier=1)
    dma("g", "w1e", [], T.w1e[:], T.en[:])
    pick8 = T.pick[:, 16:W]
    op("g", "pick", [], g.affine_select, out=pick8, in_=T.ones[:, 0:8], pattern=[[-16, 8]],
       compare_op=A.is_equal, fill=0.0, base=0, channel_multiplier=1)
    op("g", "pick16", [], g.affine_select, out=T.pick[:, 0:16], in_=T.ones[:, 0:16], pattern=[[-16, 8], [-1, 2]],
       compare_op=A.is_equal, fill=0.0, base=0, channel_multiplier=1)
    op("g", "pint", [], g.iota, out=T.pint[:], pattern=[[0, 18]], base=0, channel_multiplier=1)
    op("g", "zcol", [], g.iota, out=T.zcol[:], pattern=[[8, 2], [32, 9]], base=16 * (go % 2), channel_multiplier=0)
    op("v", "zpad", [], v.memset, ap=T.zs[:, 128:144], constant=0.0)
    op("v", "lpad", [], v.memset, ap=T.stz[:, 256:288], constant=0.0)
    for i in range(16):
        o, c = T.win1[:, 128 * i:128 * i + 128], math.exp(4.0 * (i - 15))
        if i < 10:
            op("v", "win1", ["base"], v.tensor_scalar, out=o, in0=T.base[:], scalar1=c, scalar2=None, op0=A.mult)
        else:
            op("s", "win1", ["base"], s.activation, out=o, in_=T.base[:], func=F.Copy, scale=c)

    def own_starts():
        op("p", "stt", ["stb", "ident"], p.transpose, out=T.pr0[:, 0:128], in_=T.stb[:], identity=T.ident[:])
        copy("v", "zs", ["stt", "zpad"], T.zs[:, 0:128], T.pr0[:, 0:128])
        k = CUT1[1] // 128
        for i in range(16):
            op("p", "fa1" if i < k else "fb1", ["zs"], p.transpose,
               out=T.first[:, 128 * i:128 * i + 128] if i < k else T.pr2[:, 128 * (i - k):128 * (i - k + 1)],
               in_=T.zs[:, i:i + 128], identity=T.ident[:])
        two = ((T.hp, T.dp, T.lp), (T.he, T.de, T.le))
        pair = lambda d: T.zs[:, 32 * (group[d] // 2):32 * (group[d] // 2) + 32]
        send("cl1", ["lists"], [(hs[i // 2], h[i % 2], l[group[d]], allr[8 * k + 2 * i:8 * k + 2 * i + 2])
                                for k, (h, dd, l) in enumerate(two) for i, d in enumerate(far)], "hlist")
        send("cs1", ["zs"], [(hs[i], T.hz[:], pair(far[2 * i]), allr[8 * i:8 * i + 8]) for i in range(2)], "hstart")
        send("cl2", [], [(cores[d], dd[go], l[group[d]], e[len(e) // 2 * k:len(e) // 2 * (k + 1)])
                         for k, (h, dd, l) in enumerate(two) for d, e in tod], "alist")
        send("cs2", [], [(cores[d], T.stz[:, 32 * go:32 * go + 32], pair(d), e) for d, e in tod], "astart")

    def scatter_scan(h, win, wp, ready, x, sc, at, cut, first, between=None):
        n = lambda t: t + str(h)
        c1, c2, c3 = cut
        for q, a, b, t in (("s", 0, c1, "xa"), ("s", c3, V, "xb"), ("v", c1, c2, "xa"), ("v", c2, c3, "xb")):
            if q == "v" and between and a == c1:
                between()
            if b > a:
                copy(q, n(t), ready + [wp[1]], x[:, a:b], win[:, 0:V].indirect(wp[0][:, a // 16:b // 16]))
        op("v", n("sa"), [n("xa"), first[0]], v.tensor_tensor_scan, out=sc[:, at:at + c2], data0=T.first[:, 0:c2],
           data1=x[:, 0:c2], initial=0.0, op0=A.add, op1=A.min)
        op("v", n("sb"), [n("xb"), n("sa"), first[1]], v.tensor_tensor_scan, out=sc[:, at + c2:at + V], data0=first[2],
           data1=x[:, c2:V], initial=sc[:, at + c2 - 1:at + c2], op0=A.add, op1=A.min)
        return n("sb")

    def columns(h, win, we, last, u, at, pick, out):
        for q, a, b in LAST:
            copy(q, "u%d_%d" % (h, a), [last, we[1]], u[:, at + 128 * a:at + 128 * b], win.indirect(we[0][:, 8 * a:8 * b]))
        for q, a, b in LAST:
            for i in range(a, b):
                op("p", "early" if h == 3 and i < EARLY else "sel%d" % h, ["u%d_%d" % (h, a), "pick"], p.matmul, out=out(i),
                   lhsT=u[:, at + 128 * i:at + 128 * i + 128], rhs=pick, start=True, stop=True)

    copy("v", "stb", ["st"], T.stb[:], T.sti[:])
    copy("v", "w1p", ["pm"], T.w1p[:], T.pmi[:])
    last = scatter_scan(1, T.win1, (T.w1p, "w1p"), ["win1"], T.xu1, T.xu1, 2 * V, CUT1,
                        ["fa1", "fb1", T.pr2[:, 0:V - CUT1[1]]], own_starts)
    columns(1, T.xu1[:, 2 * V:3 * V], (T.w1e, "w1e"), last, T.xu1, V, pick8, lambda i: T.pa0[:, i:128:16])
    fa = 16 * group[far[0]]
    na = 64 - fa
    og = 16 * go
    copy("v", "minef", ["sel1"], T.mine[:, fa:fa + 64], T.pa0[:, fa:fa + 64])
    copy("v", "minen", ["sel1"], T.mine[:, na:na + 64], T.pa0[:, na:na + 64])
    send("sf", ["minef"], [(hs[i], T.hu[:], T.mine[:, fa + 32 * i:fa + 32 * i + 32], allr[8 * i:8 * i + 8])
                           for i in range(2)], "hlab")
    send("sn", ["minen"], [(cores[d], T.land[:, og:og + 16], T.mine[:, 16 * group[d]:16 * group[d] + 16], e)
                           for d, e in tod], ["amate", "adir", "adir"])
    copy("v", "lown", [], T.stz[:, 2 * og:2 * og + 32], T.zs[:, 32 * (go // 2):32 * (go // 2) + 32])

    dma("y", "p2i", ["alist", "ownl"], T.p2i[:], T.dp[:])
    dma("y", "e2i", [], T.e2i[:], T.de[:])
    op("v", "pmod", ["pint"], v.tensor_scalar, out=T.pmod[:], in0=T.pint[:], scalar1=15, scalar2=None, op0=A.bitwise_and)
    op("v", "peven", [], v.tensor_scalar, out=T.peven[:], in0=T.pint[:], scalar1=15, scalar2=1, op0=A.bitwise_and,
       op1=A.logical_shift_right)
    op("v", "zero", [], v.memset, ap=T.reset[:], constant=0.0)
    op("v", "zero", [], v.memset, ap=T.reset16[:], constant=0.0)
    op("v", "zsum", ["peven", "zcol"], v.tensor_tensor, out=T.zsum[:], in0=T.peven[:], in1=T.zcol[:], op=A.add)
    copy("v", "one16", ["ones"], T.one16[:], T.ones[:, 0:2])
    op("s", "id32", ["ident"], s.activation, out=T.id32[:], in_=T.ident[:], func=F.Ln, scale=math.exp(32.0), bias=1.0)
    for o in range(2):
        op("v", "other", ["pmod"], v.tensor_scalar, out=T.other[:, o:o + 1], in0=T.pmod[:, 0:1], scalar1=o, scalar2=None,
           op0=A.not_equal)
    copy("v", "offz", ["zsum"], T.offz[:], T.zsum[:])
    op("v", "reset", ["zero"], v.memset, ap=T.reset[:, 0:4 * W:W], constant=1.0)
    op("v", "reset", [], v.memset, ap=T.reset16[:, 0:256:16], constant=1.0)
    for i in range(16):
        op("p", "qown", [], p.matmul, out=T.pa1[:, i:i + 1], lhsT=T.win1[:, 128 * i:128 * i + 128],
           rhs=T.pick[:, 16:17], start=True, stop=True)
    copy("s", "own", ["qown"], T.own[:], T.pa1[:, 0:16])

    def halves(q, name, after, win, a, b, ps):
        for o in range(2):
            out, in_, col = win[:, V // 2 * o + 128 * a:V // 2 * o + 128 * b], ps[:, 0:128 * (b - a)], T.other[:, o:o + 1]
            if q == "v":
                op(q, name, after + ["other"], v.tensor_scalar, out=out, in0=in_, scalar1=col, scalar2=None, op0=A.max)
            else:
                op(q, name, after + ["other"], s.activation, out=out, in_=in_, func=F.Identity, bias=col)

    copy("s", "twice", ["astart", "lown", "lpad", "offz"], T.twice[:], T.stz[:, 0:288].indirect(T.offz[:, 0:18]))
    labels = lambda d: T.land[:, 16 * group[d]:16 * group[d] + 16]
    side = [(t, T.mine[:, og:og + 16], "minen") for t in [0] + list(range(8, 16))] + [(1, labels(mate), "amate")]
    side += [(2 + k, labels(d), "adir") for k, d in enumerate(plane)] + [(4 + k, labels(d), "arel") for k, d in enumerate(far)]
    for t, src, after in side:
        op("p", "side", [after], p.matmul, out=T.pa2[:, t:256:16], lhsT=T.ident[:], rhs=src, start=True, stop=True)
    for o in range(2):
        op("v", "b1", ["side", "reset"], v.tensor_tensor_scan, out=T.xu1[:, o:V:16], data0=T.reset16[:, 0:128],
           data1=T.pa2[:, 128 * o:128 * o + 128], initial=0.0, op0=A.add, op1=A.min)
    copy("v", "w2p", ["p2i"], T.w2p[:], T.p2i[:])
    copy("v", "w2e", ["e2i"], T.w2e[:], T.e2i[:])
    for q, a, b, ps in ROWS:
        for i in range(a, b):
            o, l = T[ps][:, 128 * (i - a):128 * (i - a + 1)], T.xu1[:, 256 * i + 128:256 * i + 256]
            if q == "v":
                op("p", "row%d" % a, ["b1"], p.transpose, out=o, in_=l, identity=T.ident[:])
            else:
                op("p", "row%d" % a, ["b1", "own"], p.matmul, out=o, lhsT=l, rhs=T.ident[:], start=True, stop=True)
        halves(q, "win2", ["row%d" % a], T.win2, a, b, T[ps])
    for i in range(16):
        at = 144 * (i // 8) + 2 * (i % 8)
        op("p", "f2", ["twice"], p.transpose, out=T.first[:, 128 * i:128 * i + 128], in_=T.twice[:, at:at + 128],
           identity=T.ident[:])
    first = ["f2", "f2", T.first[:, CUT[1]:V]]

    last = scatter_scan(2, T.win2, (T.w2p, "w2p"), ["win2"], T.x2, T.s2, 0, CUT, first)
    names = list(BACK)

    def needs(c):
        k, x = c[0], c[1]
        out = [t + x for t in {"g": "", "h": "", "s": "gh", "m": "s", "r": "m", "c": "r"}[k]]
        if k in "sr" and names.index(x) >= 3:
            out.append({"s": "m", "r": "c"}[k] + names[names.index(x) - 3])
        return out

    def emit(q, c):
        k, x = c[0], c[1]
        a, b = BACK[x]
        n, pa, pr = b - a, T["pa%d" % (names.index(x) % 3)], T["pr%d" % (names.index(x) % 3)]
        after = ["bk" + t for t in needs(c)]
        if k in "gh":
            a, b = (a, b) if k == "g" else (a + 8, b + 8)
            copy(q, "bk" + c, [last, "w2e"], T.u2[:, 128 * a:128 * b], T.s2[:, 0:V].indirect(T.w2e[:, 8 * a:8 * b]))
        elif k == "s":
            for j, i in enumerate(list(range(a, b)) + list(range(a + 8, b + 8))):
                op(q, "bk" + c, after + ["pick16"], p.matmul, out=pa[:, W * j:W * j + W],
                   lhsT=T.u2[:, 128 * i:128 * i + 128], rhs=T.pick[:], start=True, stop=True)
        elif k == "m":
            for o in range(2):
                op(q, "bk" + c, after + ["reset"], v.tensor_tensor_scan, out=T.xu1[:, 16 * W * a + o:16 * W * b:16],
                   data0=T.reset[:, 0:W * n], data1=pa[:, W * n * o:W * n * (o + 1)], initial=0.0, op0=A.add, op1=A.min)
        elif k == "r":
            for i in range(a, b):
                op(q, "bk" + c, after, p.transpose, out=pr[:, 128 * (i - a):128 * (i - a + 1)],
                   in_=T.xu1[:, 16 * W * (i + 1) - 128:16 * W * (i + 1)], identity=T.ident[:])
        else:
            halves(q, "bk" + c if c == "ca" else "win3", after, T.win3, a, b, pr)

    weave(BACK_ORDER, needs, emit)

    last = scatter_scan(3, T.win3, (T.w2p, "w2p"), ["bkca", "win3"], T.x3, T.s3, 0, CUT, first)
    columns(3, T.s3[:, 0:V], (T.w2e, "w2e"), last, T.u3, 0, T.pick[:, 0:16],
            lambda i: (T.pa1 if i < EARLY else T.pa2)[:, 16 * i:16 * i + 16])
    for after, ps, a, b in (("early", T.pa1, 0, 16 * EARLY), ("sel3", T.pa2, 16 * EARLY, 256)):
        op("v", "m3", [after], v.tensor_tensor_scan, out=T.m3[:, a:b], data0=T.reset16[:, a:b], data1=ps[:, a:b], initial=0.0,
           op0=A.add, op1=A.min)
    tile = T.landy[:, 2 * og:2 * og + 32]
    for j in range(2):
        op("s", "yt", ["m3"], s.activation, out=T.landy[:, 2 * og + 16 * j:2 * og + 16 * j + 16:2],
           in_=T.m3[:, 15 + 16 * j:256:32], func=F.Ln, scale=math.exp(32.0))
    op("v", "yt", ["m3", "own"], v.tensor_tensor, out=T.landy[:, 2 * og + 1:2 * og + 32:2], in0=T.m3[:, 15:256:16],
       in1=T.own[:], op=A.is_equal)

    send("yf", ["yt"], [(hs[i], T.hy[:], tile, allr[8 * i:8 * i + 8]) for i in range(2)], "hfin")
    send("yn", [], [(cores[d], tile, tile, e) for d, e in tod], "aydir")

    def count(name, arrived, k0):
        for q, a, b, ps in (("s", k0, k0 + 3, T.pa2), ("v", k0 + 3, k0 + 4, T.pa1)):
            op("p", "cnt" + q + name, arrived, p.matmul, out=ps[0:1, 0:16 * (b - a)], lhsT=T.one16[:, 0:1],
               rhs=T.landy[:, 32 * a + 1:32 * b:2], start=True, stop=True)
            for k in range(a, b):
                in_, out = ps[0:1, 16 * (k - a):16 * (k - a + 1)], T.crow[0:1, k:k + 1]
                if q == "v":
                    op(q, "crow" + name, ["cnt" + q + name], v.tensor_reduce, out=out, in_=in_, axis=AxisListType.X, op=A.add)
                else:
                    op(q, "crow" + name, ["cnt" + q + name], s.activation, out=T.crun[0:1, 16 * k:16 * k + 16], in_=in_,
                       func=F.Copy, accum_out=out)

    count("n", ["aydir", "yt", "one16", "id32"], na // 16)
    count("f", ["crown", "ayrel"], fa // 16)
    op("p", "psy", ["id32"], p.matmul, out=T.pa0[0:16, 0:128], lhsT=T.landy[:, 2 * rank:256:16], rhs=T.id32[:],
       start=True, stop=True)
    op("v", "yrow", ["psy"], v.tensor_scalar, out=T.yrow[0:16, :], in0=T.pa0[0:16, 0:128], scalar1=ROUND,
       scalar2=ROUND - V // 2, op0=A.add, op1=A.subtract)
    dma("y", "yout", ["yrow"], T.y[:], T.yrow[0:16, :])
    dma("s", "cout", ["crown", "crowf"], T.cnt[:], T.crow[0:1, :])
    finish()
